import numpy as np, ml_dtypes
CORES = [6,15,38,47]
N = 4
BF = ml_dtypes.bfloat16
W, V, L, F, B, TH, S, RO, SV = 4096, 1024, 256, 3, 3, 9, 2, 3, 4
def parts(rng):
    x = np.clip(rng.integers(0, 256, (N, 8, 1, W)) + rng.integers(-70, 71, (N, 8, 16, W)), 0, 255)
    q = np.clip(rng.integers(0, 200, (N, 8, 1, L)) + rng.integers(-70, 71, (N, 8, 16, L)), 0, 255)
    return x, q, rng.integers(0, W, (N, 8, W)), rng.integers(0, W, (N, 8, W)), rng.integers(0, V, (N, 8, W)), rng.integers(0, W, (N, 8, 16, V))
def pack(x, q, nx, pv, rc, u):
    return {"xd": np.ascontiguousarray(x.reshape(N, 128, W)).astype(np.float32).astype(BF), "nx": nx.astype(np.int32), "pv": pv.astype(np.int32), "rc": rc.astype(np.int32),
            "ul": np.ascontiguousarray(u.reshape(N, 128, V)).astype(np.int32), "mv": np.ascontiguousarray(q.reshape(N, 128, L)).astype(np.float32).astype(BF)}
def some(rng, n):
    return 255 * (np.argsort(rng.random((N, 8, 16, L)), axis=2) < n[:, :, None, :])
def setup_inputs(rng):
    return pack(*parts(rng))
def setup_inputs_corners(rng):
    x, q, nx, pv, rc, u = parts(rng); c = np.arange(W); sh = int(rng.integers(0, 8))
    x[..., ::64] = 255; x[..., 63::64] = 0; q[..., :8] = 0; q[..., L - 8:] = 255
    for r in range(N):
        for g in range(8):
            k = (g + 3 * r + sh) % 8
            if k == 0: nx[r, g] = c; pv[r, g] = c; rc[r, g] = c % V
            elif k == 1: nx[r, g] = np.minimum(c + 1, W - 1); pv[r, g] = np.maximum(c - 1, 0); rc[r, g] = V - 1 - c % V
            elif k == 2: nx[r, g] = (c + 1) % W; pv[r, g] = (c + W - 1) % W
            elif k == 3: nx[r, g] = 0; pv[r, g] = W - 1; rc[r, g] = V - 1
            elif k == 4: nx[r, g] = W - 1; pv[r, g] = 0; rc[r, g] = 0
            elif k == 5: u[r, g] = u[r, g, :1] + np.zeros((16, 1), np.int64)
            elif k == 6: u[r, g] = rng.choice(np.array([0, W - 1, W // 2]), (16, V))
            else: nx[r, g] = c ^ 1; pv[r, g] = c ^ 1
            if (g + r) % 2 == 0:
                z, p, e, t1, t2, t3 = [int(b) for b in 1 + rng.permutation(W - 2)[:6]]; xb, ub, i = x[r, g], u[r, g], int(rng.integers(0, 16))
                xb[:, [z, p]] = 0; xb[i, p] = 1; xb[:, [e, t1, t2, t3]] = 255; xb[i, e] = 254
                nx[r, g, [z, p, t1, t2, t3]] = z; pv[r, g, [z, t1, t3]] = t1; pv[r, g, [p, e, t2]] = t2
                ub[:, (L - 1) * SV] = p; ub[15, (L - 1) * SV] = z
                ub[:, (L - 2) * SV] = t3
                ub[:, SV] = t1; ub[15, SV] = e
    return pack(x, q, nx, pv, rc, u)
def setup_inputs_counts(rng):
    x, q, nx, pv, rc, u = parts(rng); x = np.clip(x, 1, 254)
    much = rng.permutation(np.array((256, 511, 1024, 8 * L - 1, 255, 257, 8 * L, 0)[:N]))
    hit = (np.argsort(rng.random((N, 8 * L)), axis=1) < much[:, None]).reshape(N, 8, L)
    n = np.where(hit, rng.integers(TH, 17, (N, 8, L)), rng.integers(0, TH, (N, 8, L)))
    return pack(x, some(rng, n), nx, pv, rc, u)
def setup_inputs_ends(rng):
    x = 255 * rng.integers(0, 2, (N, 8, 16, W)); m = rng.random((N, 8, 1, W)); x = np.where(m < 0.3, 0, np.where(m < 0.6, 255, x))
    fl = rng.integers(0, 2, (N, 8)); fl[0] = 0; fl[N - 1] = 0; f2 = rng.integers(0, 2, (N, 8))
    x[:, :, :, 0] = 255 * fl[:, :, None]; x[:, :, :, W - 1] = 255 * (1 - fl)[:, :, None]
    odd = (np.arange(8) % 2 == 1)[None, :, None]
    def far(hi, n):
        a = hi * rng.integers(0, 2, (N, 8, n))
        return np.where((rng.random((N, 8, n)) < 0.35) & odd, rng.integers(0, hi + 1, (N, 8, n)), a)
    nx = far(W - 1, W); pv = far(W - 1, W); rc = far(V - 1, W); u = far(W - 1, 16 * V).reshape(N, 8, 16, V)
    u[N - 1] = (W - 1) * rng.integers(0, 2, (8, 16, V)); nx[N - 1, :, 0] = 0; nx[N - 1, :, W - 1] = 0
    rc[:, :, 0] = (V - 1) * f2; rc[:, :, W - 1] = (V - 1) * (1 - f2)
    n = rng.choice(np.array([0, TH - 1, TH, 16]), (N, 8, L))
    n[0] = rng.choice(np.array([0, TH - 1, TH // 2]), (8, L)); n[N - 1] = rng.choice(np.array([16, TH]), (8, L))
    z = (L - 1) * SV; n[0, 7, L - 2:] = 0; n[N - 1, 7, L - 1] = 16
    u[0, 7, :, z] = W - 1; u[0, 7, :, z - SV] = W - 1; u[0, 7, 15, z - SV] = 0
    u[N - 1, 7, :, z] = W - 1; u[N - 1, 7, 15, z] = 0
    n[1, 7, L - 1] = 16; x[1, 7, :, 0] = 0; x[1, 7, :, 1] = 255; x[1, 7, :, 2] = 0; x[1, 7, :, W - 1] = 255
    nx[1, 7, 0] = W - 1; nx[1, 7, W - 1] = W - 1; nx[1, 7, 1] = 2; u[1, 7, :15, z] = 1; u[1, 7, 15, z] = 0
    return pack(x, some(rng, n), nx, pv, rc, u)
def setup_inputs_near(rng):
    x, q, nx, pv, rc, u = parts(rng); b = rng.integers(0, 255, (N, 8, 1, 1)); b[0, 0] = 0; b[1, 1] = 254
    x = b + (rng.random((N, 8, 16, W)) < rng.choice(np.array([0.2, 0.5, 0.8]), (N, 8, 1, W)))
    q = b + (rng.random((N, 8, 16, L)) < rng.choice(np.array([0.2, 0.5, 0.8, 1.0]), (N, 8, 1, L)))
    few = rng.integers(0, W, (N, 8, 64)); u = np.take_along_axis(few, rng.integers(0, 64, (N, 8, 16 * V)), 2).reshape(N, 8, 16, V)
    return pack(x, q, nx, pv, rc, u)
def setup_inputs_spread(rng):
    x = (np.exp2(8 * rng.random((N, 8, 1, W))) * rng.random((N, 8, 16, W))).astype(np.int64)
    q = (np.exp2(8 * rng.random((N, 8, 1, L))) * rng.random((N, 8, 16, L))).astype(np.int64)
    def skew(hi, n):
        return np.minimum((hi * rng.random((N, 8, n)) ** rng.choice(np.array([1, 2, 4]), (N, 8, 1))).astype(np.int64), hi - 1)
    return pack(np.minimum(x, 255), np.minimum(q, 255), skew(W, W), skew(W, W), skew(V, W), skew(W, 16 * V).reshape(N, 8, 16, V))
def check_inputs(d):
    bad = []
    for k, lo, hi in (("xd", 0, 255), ("nx", 0, W - 1), ("pv", 0, W - 1), ("rc", 0, V - 1), ("ul", 0, W - 1), ("mv", 0, 255)):
        a = np.asarray(d[k]).astype(np.float64)
        if not (np.min(a) >= lo and np.max(a) <= hi): bad.append("range of " + k)
        elif np.any(a != np.floor(a)): bad.append("whole numbers in " + k)
    return bad
def lowest(n):
    same = n[:, :, :, None] == n[:, :, None, :]
    return ~np.any(same & np.tril(np.ones((L, L), bool), -1), axis=3)
def reference(xd, nx, pv, rc, ul, mv):
    X = np.ascontiguousarray(xd.astype(np.float32).astype(np.int32).reshape(N, 8, 16, W).transpose(0, 1, 3, 2))
    q = np.ascontiguousarray(mv.astype(np.float32).astype(np.int32).reshape(N, 8, 16, L).transpose(0, 1, 3, 2))
    nxt, pre, rec = nx.astype(np.int64), pv.astype(np.int64), rc.astype(np.int64)
    U = ul.astype(np.int64).reshape(N, 8, 16, V); v = np.zeros((N, 8, L), np.int64) + SV * np.arange(L)
    R3, G3 = np.arange(N)[:, None, None], np.arange(8)[None, :, None]; R4, G4 = R3[..., None], G3[..., None]
    for t in range(RO):
        d = np.take_along_axis(U, v[:, :, None, :], 3)
        score = np.add.reduce(np.abs(X[R4, G4, d] - q[:, :, None]), axis=4)
        cleared = np.zeros(d.shape, bool); c = d
        for f in range(F):
            c = nxt[R4, G4, c]
            cleared = cleared | (np.add.reduce((X[R4, G4, c] < q[:, :, None]).astype(np.int32), axis=4) >= TH)
        none = np.all(cleared, axis=2)
        k = np.where(none, np.argmax(score, axis=2), np.argmin(np.where(cleared, 2 ** 20, score), axis=2))
        a = np.take_along_axis(d, k[:, :, None, :], 2)[:, :, 0]; go = np.ones(a.shape, bool)
        for s in range(B):
            b = pre[R3, G3, a]
            go = go & (np.add.reduce((X[R3, G3, b] < q).astype(np.int32), axis=3) < TH)
            a = np.where(go, b, a)
        w = rec[R3, G3, a]
        A = np.add.reduce(none.reshape(N, -1).astype(np.int32), axis=1) & 255
        z = (q + A[:, None, None, None]) >> 1
        xn = (X[R3, G3, a] + q + 1) >> 1; nn = nxt[R3, G3, nxt[R3, G3, a]]
        r, g, i = np.nonzero(lowest(v)); U[r, g, k[r, g, i], v[r, g, i]] = a[r, g, i]
        r, g, i = np.nonzero(lowest(a)); X[r, g, a[r, g, i]] = xn[r, g, i]; nxt[r, g, a[r, g, i]] = nn[r, g, i]
        v = w + 0; q = z + 0
        for h in range(1, S):
            s = 1 + (t + h - 1) % (N - 1)
            v[:, :, h::S] = np.roll(w, s, axis=0)[:, :, h::S]; q[:, :, h::S] = np.roll(z, s, axis=0)[:, :, h::S]
    return {"yu": U.reshape(N, 128, V).astype(np.float32), "yx": np.ascontiguousarray(X.transpose(0, 1, 3, 2)).reshape(N, 128, W).astype(np.float32).astype(BF),
            "yv": v.astype(np.float32), "yq": np.ascontiguousarray(q.transpose(0, 1, 3, 2)).reshape(N, 128, L).astype(np.float32).astype(BF)}

@@ -1,0 +1,592 @@
+from concourse.mybir import dt, AluOpType, AxisListType, ActivationFunctionType
+
+RO = 3
+BIG = 131072.0
+F32, BF, I32, U16 = "float32", "bfloat16", "int32", "uint16"
+SB = {
+    "X": (4352, BF), "M": (4352, BF), "U": (1280, F32), "UI": (1024, I32), "PV1": (4096, F32), "RC1": (4096, F32),
+    "IO1": (4096, F32),
+    "nxd": (256, I32), "pvd": (256, I32), "rcd": (256, I32), "pvf": (256, F32), "rcf": (256, F32),
+    "nxh": (256, I32), "nxl": (256, I32), "nhb": (256, BF), "nlb": (256, BF),
+    "PI": (1, I32), "PRi": (1, I32), "PGi": (1, I32), "PIf": (1, F32), "PR": (1, F32), "PG": (1, F32), "WT": (1, F32), "WT2": (1, F32),
+    "XR": (256, F32), "GR": (128, F32), "CI": (128, F32), "DW0": (16, F32), "DWA": (16, F32), "DWV": (16, F32), "VL0": (16, U16),
+    "MK": (128, F32), "MK2": (256, F32), "DX1": (256, F32), "DX2": (256, F32), "DX": (256, F32), "P3": (1, F32), "P4": (1, F32), "SC1": (1, F32), "SC8": (1, F32), "INV": (1, F32),
+    "BQ": (128, BF), "N4V": (256, F32), "N4A": (256, F32), "VU": (16, F32), "HU": (16, F32), "BO": (128, BF), "BW": (128, BF), "LK": (2048, BF), "LB": (2048, BF), "I16": (128, BF), "NI": (128, BF), "IF": (128, F32),
+    "G8": (8, BF), "G8S": (8, BF), "R8": (8, F32), "N8S": (8, BF), "KC1": (128, BF), "KC2": (128, BF), "P0": (1, F32), "P1": (1, F32), "P2": (1, F32), "NAT": (256, F32), "DS": (128, F32), "DMIN": (128, F32), "ONES": (128, BF),
+    "AW": (16, F32), "NB": (16, BF), "NR": (1, F32), "NRi": (1, I32), "NA": (1, I32), "AH": (1, F32), "ZI": (256, I32),
+    "DL": (256, U16), "DF": (256, F32), "QX": (4096, BF), "VN": (256, F32), "VM": (256, F32), "VS": (256, F32), "V16": (256, U16), "VL": (16, U16),
+    "VA": (16, U16), "CMV": (256, F32), "WCV": (256, F32), "TV1": (16, F32), "TV2": (16, F32), "TV3": (16, F32), "EQV": (2048, BF), "EDV": (128, BF),
+    "CMA": (256, F32), "WCA": (256, F32), "TA1": (16, F32), "TA2": (16, F32), "TA3": (16, F32), "ADR": (16, U16),
+    "AL": (16, U16), "A16": (256, U16), "A1M": (256, F32), "A1S": (256, F32), "ND": (256, F32), "UV": (256, F32), "UT": (256, F32), "XS": (256, F32), "XN": (256, I32),
+    "NP": (256, BF), "NNP": (256, BF), "NLA": (16, U16), "YV": (256, F32),
+}
+for _h in range(2):
+    for _n, _v in {"XG": (2048, BF), "AB": (2048, BF), "IGa": (2048, BF), "IGb": (2048, BF), "NLa": (128, U16), "NLb": (128, U16), "NLc": (128, U16),
+                   "LWa": (2048, BF), "LWb": (2048, BF), "M1": (128, F32), "M2": (128, F32), "M3": (128, F32), "CL": (128, F32), "S1": (128, F32), "AT": (128, F32), "UU": (128, F32), "KEY": (128, F32), "SCN": (128, F32), "W2": (128, F32), "ASU": (128, F32),
+                   "OHT": (128, BF), "OHS": (128, F32), "NOH": (128, F32), "DT": (128, F32), "AM": (128, F32), "AL0": (8, U16), "AL1": (8, U16), "AL2": (8, U16), "AL3": (8, U16),
+                   "WM1": (128, F32), "WM2": (128, F32), "WM3": (128, F32), "WS1": (128, F32), "WS2": (128, F32), "WS3": (128, F32), "LQ": (384, BF),
+                   "HG": (32, F32), "HD": (32, F32), "HS": (32, F32), "EQA": (2048, BF), "EDA": (128, BF)}.items():
+        SB[_n + str(_h)] = _v
+for _t in range(2):
+    SB["Q%d" % _t] = (256, BF)
+SB["WB"] = (256 * RO, F32)
+SB["RV"] = (256 * RO, F32)
+SB["ZB"] = (256 * RO, BF)
+SB["RZ"] = (256 * RO, BF)
+POOL, SIZE = {}, {}
+SAME = {"XN": "nxh", "ZI": "nxl", "WCV": "pvf", "N4V": "rcf", "N4A": "DX1", "VS": "DX2", "VN": "MK2", "NP": "nhb", "NNP": "nlb", "EQV": "EQA0"}
+for _n, (_c, _d) in sorted(SB.items(), key=lambda e: e[0] in SAME):
+    if _n in ("WB", "RV", "ZB", "RZ"):
+        continue
+    if _n in SAME:
+        POOL[_n] = POOL[SAME[_n]]
+        continue
+    _o = SIZE.get(_d, 0)
+    POOL[_n] = ("p" + _d, _o)
+    SIZE[_d] = _o + (_c + 15) // 16 * 16
+SCRATCH = {"p" + _d: ("sbuf", [128, _c], _d) for _d, _c in SIZE.items()}
+for _n in ("WB", "RV", "ZB", "RZ"):
+    SCRATCH[_n] = ("sbuf", [128, SB[_n][0]], SB[_n][1])
+for _i in range(8):
+    SCRATCH["ps%d" % _i] = ("psum", [128, 512], F32)
+NDMA = 24
+SEMAPHORES = ["qv", "qs", "qt", "qg", "ls"] + ["d%d" % i for i in range(NDMA)] + ["r%s%d" % (a, t) for a in "abz" for t in range(RO)]
+BYTES = {F32: 4, I32: 4, BF: 2, U16: 2}
+GC, SCC, CY = 1.5, 3.6, 0.83 * 1.2
+HOP = 70.0
+SMODE = ("v", "v")
+HINT = {"0": 15000.0}
+QXS = "vss"
+XLATE = True
+CH = 64
+
+
+def rank_program(g, core, T, topo):
+    rank = T.rank_of(core)
+    if rank is None:
+        return
+    A, F, X = AluOpType, ActivationFunctionType, AxisListType.X
+    V, Sc, Te = g.vector, g.scalar, g.tensor
+    nodes, acc, ndma, HUE, turn = [], {}, [0], [2], [0]
+
+    def R(n, a=0, b=None, s=1):
+        if n in POOL:
+            p, o = POOL[n]
+            return (p, o + a, o + (SB[n][0] if b is None else b), s, n)
+        return (n, a, SCRATCH[n][1][-1] if b is None else b, s, n)
+
+    def IND(n, w, l, c=0, d=None):
+        return ("ind", R(n, 0, w), R(l, c, d))
+
+    def ap(r):
+        if r[0] == "ind":
+            return ap(r[1]).indirect(ap(r[2]))
+        t = T[r[0]]
+        if len(SCRATCH[r[0]][1]) == 3:
+            return t[:, :, r[1]:r[2]]
+        return t[:, r[1]:r[2]] if r[3] == 1 else t[:, r[1]:r[2]:r[3]]
+
+    def cnt(r):
+        if r[0] == "ind":
+            return 16 * (r[2][2] - r[2][1])
+        k = (r[2] - r[1] + r[3] - 1) // r[3]
+        return k * 8 if len(SCRATCH[r[0]][1]) == 3 else k
+
+    def two(r):
+        r = r[1] if r[0] == "ind" else r
+        return BYTES[SCRATCH[r[0]][2]] == 2
+
+    def meet(a, b):
+        if a[1] >= b[2] or b[1] >= a[2]:
+            return False
+        return not (a[3] == b[3] and a[3] > 1 and (a[1] - b[1]) % a[3])
+
+    def node(q, calls, reads, writes, cost, lat=0.0, after=(), ahead=(), **kw):
+        i = len(nodes)
+        need, order = set(after), set(ahead)
+        touch = []
+        for r in reads:
+            touch += [(r[1], False), (r[2], False)] if r[0] == "ind" else [(r, False)]
+        for w in writes:
+            touch += [(w[1], True), (w[2], False)] if w[0] == "ind" else [(w, True)]
+        for r, wr in touch:
+            for j, r2, wr2 in acc.setdefault(r[0], []):
+                if j == i:
+                    continue
+                bank = r[0][:2] == "ps" and nodes[j]["q"] != q
+                if bank or ((wr or wr2) and meet(r, r2)):
+                    if nodes[j]["q"] == q and q == "t" and wr2 and wr:
+                        order.add(j)
+                    else:
+                        need.add(j)
+                elif r[0][:2] == "ps" and wr and wr2:
+                    order.add(j)
+        for r, wr in touch:
+            L = acc[r[0]]
+            if wr and r[3] == 1:
+                L[:] = [e for e in L if not (e[1][1] >= r[1] and e[1][2] <= r[2] and (r[0][:2] != "ps"))]
+            if r[0][:2] == "ps" and len(L) > 60:
+                del L[:20]
+            L.append((i, r, wr))
+        nodes.append(dict(q=q, calls=calls, need=need, order=order - need, cost=cost, lat=lat, lab="%s%d%s" % (q, HUE[0], (writes[0][1] if writes[0][0] == "ind" else writes[0])[4] if writes else ""), **kw))
+        return i
+
+    def vcost(o, ins, per):
+        n = cnt(o)
+        if o[0] == "ind":
+            return 50 + n * SCC * CY
+        for r in ins:
+            if r[0] == "ind":
+                return 50 + n * GC * CY
+        if per == 1 and two(o) and all(two(r) for r in ins):
+            per = 0.5
+        if per == 2 and any(r[0][:2] == "ps" for r in ins):
+            per = 1
+        return max(64, n * per) * CY
+
+    def bundle(q, items):
+        return node(q, [c for c, _, _, _ in items], [r for _, rs, _, _ in items for r in rs], [w for _, _, ws, _ in items for w in ws],
+                    sum(c for _, _, _, c in items))
+
+    def i_copy(o, i):
+        return (lambda: V.tensor_copy(ap(o), ap(i)), [i], [o], vcost(o, [i], 1))
+
+    def i_tt(o, a, b, op):
+        return (lambda: V.tensor_tensor(ap(o), ap(a), ap(b), op), [a, b], [o], vcost(o, [a, b], 2))
+
+    def i_ts(o, a, s1, s2, op0, op1=None):
+        rs = [a] + [s for s in (s1, s2) if isinstance(s, tuple)]
+
+        def call():
+            x1 = ap(s1) if isinstance(s1, tuple) else s1
+            x2 = ap(s2) if isinstance(s2, tuple) else s2
+            if op1 is None:
+                return V.tensor_scalar(ap(o), ap(a), x1, None, op0)
+            return V.tensor_scalar(ap(o), ap(a), x1, x2, op0, op1)
+        return (call, rs, [o], vcost(o, [a], 1))
+
+    def i_set(o, v):
+        return (lambda: V.memset(ap(o), v), [], [o], vcost(o, [], 1))
+
+    def vcopy(o, i):
+        return bundle("v", [i_copy(o, i)])
+
+    def vtt(o, a, b, op):
+        return bundle("v", [i_tt(o, a, b, op)])
+
+    def vts(o, a, s1, s2, op0, op1=None):
+        return bundle("v", [i_ts(o, a, s1, s2, op0, op1)])
+
+    def vset(o, v):
+        return bundle("v", [i_set(o, v)])
+
+    def vscan(o, d0, d1, op0, op1):
+        return node("v", [lambda: V.tensor_tensor_scan(ap(o), ap(d0), ap(d1), 0.0, op0, op1)], [d0, d1], [o], vcost(o, [d0], 1))
+
+    def i_act(o, i, f, bias=0.0, scale=1.0):
+        n = cnt(o)
+        c = 65 + n * GC * CY if i[0] == "ind" else max(64, n) * CY
+        return (lambda: Sc.activation(ap(o), ap(i), f, bias=bias, scale=scale), [i], [o], c)
+
+    def sact(o, i, f, bias=0.0, scale=1.0):
+        return bundle("s", [i_act(o, i, f, bias, scale)])
+
+    def pe(mms, x4=1):
+        def call(m):
+            return lambda: Te.matmul(ap(m[0]), ap(m[1]), ap(m[2]), m[3], m[4])
+        return node("t", [call(m) for m in mms], [m[k] for m in mms for k in (1, 2)], [m[0] for m in mms],
+                    sum(max(64, cnt(m[2])) * x4 * CY for m in mms))
+
+    def dma(q, pairs, reads, writes, nbytes, then=None):
+        k = ndma[0]
+        ndma[0] += 1
+        e = g.sync if q == "y" else Sc
+
+        def call(o, i):
+            return lambda: e.dma_start(o(), i())
+        return node(q, [call(o, i) for o, i in pairs], reads, writes, 60.0 * len(pairs), 2000.0 + nbytes / 200.0, ahead=() if then is None else (then,), dsem="d%d" % k, tot=16 * len(pairs))
+
+    def iota(o, pat, base, cm):
+        n = cnt(o)
+        i32 = SCRATCH[o[0]][2] == I32
+        return node("g", [(lambda: g.iota(ap(o), pat, base, cm)) if i32 else (lambda: g.iota(ap(o), pat, base, cm, allow_small_or_imprecise_dtypes=True))],
+                    [], [o], 130 + n * 2 * CY)
+
+    dma("y", [(lambda: ap(R("nxd")), lambda: T.nx[:, :])], [], [R("nxd")], 131072)
+    dma("s", [(lambda: ap(R("UI")), lambda: T.ul[:, :])], [], [R("UI")], 524288)
+    dma("y", [(lambda: ap(R("Q0")), lambda: T.mv[:, :])], [], [R("Q0")], 65536)
+    vset(R("M", 0, 4096), 0.0)
+    bundle("v", [i_ts(R("nxh"), R("nxd"), 4, None, A.arith_shift_right), i_ts(R("nxl"), R("nxd"), 15, None, A.bitwise_and)])
+    bundle("v", [i_copy(R("nhb"), R("nxh")), i_copy(R("nlb"), R("nxl"))])
+    pm, om = POOL["M"]
+    i = dma("y", [(lambda: T[pm][0:128:16, om:om + 4096], lambda: ap(R("nhb"))), (lambda: T[pm][1:128:16, om:om + 4096], lambda: ap(R("nlb")))],
+            [R("nhb"), R("nlb")], [R("M", 0, 4096)], 131072)
+    j = i if XLATE else None
+    j = dma("y", [(lambda: ap(R("X", 0, 4096)), lambda: T.xd[:, :])], [], [R("X", 0, 4096)], 1048576, j)
+    dma("y", [(lambda: ap(R("pvd")), lambda: T.pv[:, :])], [], [R("pvd")], 131072, j)
+    j = dma("y", [(lambda: ap(R("rcd")), lambda: T.rc[:, :])], [], [R("rcd")], 131072, j)
+    iota(R("PI"), [[0, 1]], 0, 1)
+    iota(R("PIf"), [[0, 1]], 0, 1)
+    iota(R("GR"), [[1, 8], [0, 16]], 0, 0)
+    iota(R("XR"), [[0, 16], [1, 16]], 0, 0)
+    iota(R("CI"), [[1, 128]], 0, 0)
+    iota(R("DW0"), [[16, 16]], 0, 0)
+    iota(R("IO1"), [[1, 4096]], 1, 0)
+    bundle("v", [i_ts(R("PRi"), R("PI"), 15, None, A.bitwise_and), i_ts(R("PGi"), R("PI"), 4, None, A.arith_shift_right)])
+    bundle("v", [i_copy(R("PR"), R("PRi")), i_copy(R("PG"), R("PGi"))])
+    bundle("v", [i_ts(R("WT"), R("PR"), 0.0, 16.0, A.is_equal, A.mult), i_ts(R("WT2"), R("PR"), 1.0, None, A.is_equal)])
+    vtt(R("WT"), R("WT"), R("WT2"), A.add)
+    vts(R("BW"), R("GR"), R("PG"), R("WT"), A.is_equal, A.mult)
+    vset(R("LK"), 0.0)
+    bundle("v", [i_copy(R("LK", 128 * k + k, 128 * k + 128, 16), R("BW", k, 128, 16)) for k in range(16)])
+    vts(R("BO"), R("GR"), R("PG"), None, A.is_equal)
+    vset(R("LB"), 0.0)
+    bundle("v", [i_copy(R("LB", 128 * k + k, 128 * k + 128, 16), R("BO", k, 128, 16)) for k in range(16)])
+    vts(R("I16"), R("CI"), R("PIf"), None, A.is_equal)
+    vts(R("NI"), R("CI"), R("PIf"), -1.0, A.is_equal, A.mult)
+    vts(R("IF"), R("CI"), R("PIf"), None, A.is_equal)
+    vts(R("G8"), R("CI", 0, 8), R("PG"), None, A.is_equal)
+    vts(R("G8S"), R("CI", 0, 8), R("PG"), 16.0, A.is_equal, A.mult)
+    vts(R("R8"), R("CI", 0, 8), R("PG"), None, A.is_equal)
+    vts(R("MK"), R("XR", 0, 128), R("PR"), None, A.is_equal)
+    bundle("v", [i_ts(R("P0"), R("PIf"), 0.0, None, A.is_equal), i_ts(R("P1"), R("PIf"), 1.0, BIG, A.is_equal, A.mult), i_ts(R("P2"), R("PIf"), 2.0, 65280.0, A.is_equal, A.mult)])
+    vtt(R("P1"), R("P1"), R("P2"), A.add)
+    vts(R("KC1"), R("XR", 0, 128), R("P0"), None, A.mult)
+    vts(R("KC2"), R("XR", 0, 128), R("P0"), R("P1"), A.mult, A.add)
+    vts(R("N8S"), R("CI", 0, 8), R("PG"), -16.0, A.is_equal, A.mult)
+    vts(R("MK2"), R("XR"), R("PR"), None, A.subtract)
+    bundle("v", [i_ts(R("DX1"), R("MK2"), 1.0, 4095.0, A.is_equal, A.mult), i_ts(R("DX2"), R("MK2"), 1.0, None, A.is_ge)])
+    vtt(R("DX"), R("DX1"), R("DX2"), A.add)
+    bundle("v", [i_ts(R("P3"), R("PR"), 15.0, 1.0 - 1.0 / 4096, A.is_equal, A.mult), i_ts(R("P4"), R("PR"), 15.0, 4095.0, A.is_lt, A.mult)])
+    bundle("v", [i_ts(R("SC1"), R("P3"), 1.0 / 4096, None, A.add), i_ts(R("INV"), R("P4"), 1.0, None, A.add), i_ts(R("SC8"), R("P3"), 1.0 / 4096, 8192.0, A.add, A.mult)])
+    vts(R("BQ"), R("GR"), R("PG"), 0.0625, A.is_equal, A.mult)
+    vts(R("DS"), R("XR", 0, 128), 0.0, None, A.not_equal)
+    vts(R("DMIN"), R("DS"), -1048576.0, 1048575.0, A.mult, A.add)
+    vset(R("ONES"), 1.0)
+    vts(R("DWA"), R("DW0"), R("PR"), 4097.0, A.add, A.add)
+    vts(R("DWV"), R("DW0"), R("PR"), 1025.0, A.add, A.add)
+    vts(R("VL0"), R("DW0"), R("PR"), 4.0, A.add, A.mult)
+    for h in range(2):
+        vset(R("HG%d" % h), 0.0)
+    for n, d, f in (("PV1", "pvd", "pvf"), ("RC1", "rcd", "rcf")):
+        vts(R(f), R(d), 1.0, None, A.add)
+        p, o = POOL[n]
+
+        def dst(p, o, i):
+            return lambda: T[p][i:128:16, o:o + 4096]
+        dma("y", [(dst(p, o, i), (lambda f: lambda: ap(R(f)))(f)) for i in range(16)], [R(f)], [R(n)], 2097152, j)
+    vts(R("U", 0, 1024), R("UI"), 1.0, None, A.add)
+
+    def own(o, i):
+        n = cnt(i)
+        vscan(o, R("DX", 0, n), i, A.mult, A.max)
+
+    def dedupe(nat16, scal, ed, eq, bank, base, h, natd, pref):
+        c0 = 128 * h
+        first = []
+        ms = list(range(0, 8 * h + 7))
+        full = [m for m in ms if m < 8 * h]
+        part = [m for m in ms if m >= 8 * h]
+
+        def eqs(l):
+            its = []
+            for m in l:
+                b = max(0, 16 * (m + 1) - c0)
+                its.append(i_ts(R(eq, 128 * m + b, 128 * m + 128), R(nat16, c0 + b, c0 + 128), scal(m), None, A.is_equal))
+            bundle("v", its)
+
+        def mm(m, st, sp):
+            b = max(0, 16 * (m + 1) - c0)
+            return (R(bank, base + c0 + b, base + c0 + 128), R("BO"), R(eq, 128 * m + b, 128 * m + 128), st, sp)
+        if full:
+            eqs(full)
+        reg = R(bank, base + c0, base + c0 + 128)
+        pe([(reg, R("BQ"), R("ONES"), True, False)] + [mm(m, False, False) for m in full])
+        eqs(part)
+        vtt(R(ed), natd, pref, A.is_equal)
+        pe([(reg, R("BO"), R(ed), False, False)] + [mm(m, False, m == part[-1]) for m in part])
+
+    def target(c0, c1, bank, base, wc, t1, t2, t3, aw, dw, out):
+        l0, l1 = 16 * c0, 16 * c1
+        own(R(wc, l0, l1), R(bank, base + l0, base + l1))
+        vts(R(t1, c0, c1), R(wc, l0 + 15, l1, 16), R("SC8"), -8192.0, A.mult, A.add)
+        vtt(R(t2, c0, c1), R(t1, c0, c1), R(dw, c0, c1), A.min)
+        vtt(R(t3, c0, c1), R(t2, c0, c1), aw(c0, c1), A.max)
+        vts(R(out, c0, c1), R(t3, c0, c1), -1.0, None, A.add)
+
+    recv = {}
+
+    def send(name, buf, a, b, rbuf, t):
+        dst = T.cores[(rank + 1 + t % 3) % 4]
+        rid, pid = topo.addr(dst)[0:2]
+        src = T.cores[(rank - 1 - t % 3) % 4]
+        i = node("g", [lambda: g.remote_dma(T[rbuf][:, a:b], T[buf][:, a:b], T.sem["r%s%d" % (name, t)], T.sem.ls, pid=pid, routing_id=rid, dma_engine_mask=topo.mask(core, dst))],
+                 [R(buf, a, b)], [], 900.0, remote=len(topo.engines(core, dst)))
+        recv[name, t] = node("net", [], [], [R(rbuf, a, b)], 0.0, 3500.0, after=(i,), rsem="r%s%d" % (name, t), tot=len(topo.engines(src, core)))
+
+    for t in range(RO):
+        Q, QP = "Q%d" % (t % 2), "Q%d" % ((t + 1) % 2)
+        o = 256 * (t - 1)
+        if t == 0:
+            for h in range(2):
+                vcopy(R("DL", 128 * h, 128 * h + 128), R("UI", 512 * h, 512 * h + 512, 4))
+                vts(R("DF", 128 * h, 128 * h + 128), R("UI", 512 * h, 512 * h + 512, 4), 1.0, None, A.add)
+            VA = "VL0"
+        else:
+            VA = "VA"
+            for h in range(2):
+                a, b = 128 * h, 128 * h + 128
+                HUE[0] = h
+                bundle("s", [i_act(R("VN", a, b, 2), R("WB", o + a, o + b, 2), F.Copy), i_act(R("VN", a + 1, b, 2), R("RV", o + a + 1, o + b, 2), F.Copy)])
+                own(R("VS", a, b), R("VN", a, b))
+                vts(R("VL", 8 * h, 8 * h + 8), R("VS", a + 15, b, 16), R("SC1"), -1.0, A.mult, A.add)
+                vts(R("VU", 8 * h, 8 * h + 8), R("VS", a + 15, b, 16), R("SC1"), None, A.mult)
+                vts(R("DL", a, b), IND("U", 1024, "VL", 8 * h, 8 * h + 8), -1.0, None, A.add)
+                sact(R("DF", a, b), IND("U", 1024, "VL", 8 * h, 8 * h + 8), F.Copy)
+            for h in range(2):
+                a, b = 128 * h, 128 * h + 128
+                HUE[0] = h
+                bundle("s", [i_act(R(Q, a, b, 2), R("ZB", o + a, o + b, 2), F.Copy), i_act(R(Q, a + 1, b, 2), R("RZ", o + a + 1, o + b, 2), F.Copy)])
+        for h in range(2):
+            HUE[0] = h
+            if QXS[t] == "s":
+                bundle("s", [i_act(R("QX", 2048 * h + k, 2048 * h + 2048, 16), R(Q, 128 * h, 128 * h + 128), F.Copy) for k in range(16)])
+            else:
+                bundle("v", [i_copy(R("QX", 2048 * h + k, 2048 * h + 2048, 16), R(Q, 128 * h, 128 * h + 128)) for k in range(16)])
+        if t > 0:
+            HUE[0] = 2
+            for h in range(2):
+                a, b = 128 * h, 128 * h + 128
+                sact(R("N4V", a, b), R("VN", a, b), F.Copy, scale=4096.0)
+                vcopy(R("V16", a, b), R("VN", a, b))
+                dedupe("V16", lambda m: R("VU", m, m + 1), "EDV", "EQV", "ps7", 256, h, R("N4V", a, b), R("VS", a, b))
+            target(0, 16, "ps7", 256, "WCV", "TV1", "TV2", "TV3", lambda c0, c1: R("VU", c0, c1), "DWV", "VA")
+        cb = lambda h: "ps%d" % (4 + h)
+
+        def score(h, part):
+            for w, (kc, g8) in enumerate((("KC1", "G8S"), ("KC2", "N8S"))):
+                c = 128 * w
+                pe([(R(cb(h), c, c + 128), R("ONES"), R(kc), True, False)] +
+                   [(R(cb(h), c + k, c + 128, 16), part(k), R(g8), False, k == 15) for k in range(16)])
+        for f in range(4):
+            for h in range(2):
+                HUE[0] = h
+                lst = (IND("X", 4096, "DL", 128 * h, 128 * h + 128) if f == 0 else IND("X", 4096, "NL%s%d" % ("abc"[f - 1], h)))
+                if f == 1:
+                    d = IND("X", 4096, "DL", 128 * h, 128 * h + 128)
+                    if SMODE[h] == "s":
+                        sact(R("XG%d" % h), d, F.Copy)
+                        for c in range(4):
+                            bk = ("ps2", "ps3", "ps6")[turn[0] % 3]
+                            turn[0] += 1
+                            mm = []
+                            for kk in range(4):
+                                reg = R(bk, 128 * kk, 128 * kk + 128)
+                                mm += [(reg, R("I16"), R("XG%d" % h, 4 * c + kk, 2048, 16), True, False), (reg, R("NI"), R(Q, 128 * h, 128 * h + 128), False, True)]
+                            pe(mm)
+                            sact(R("AB%d" % h, 512 * c, 512 * c + 512), R(bk), F.Abs)
+                        score(h, lambda k: R("AB%d" % h, 128 * k, 128 * k + 128))
+                    else:
+                        vtt(R("XG%d" % h), d, R("QX", 2048 * h, 2048 * h + 2048), A.subtract)
+                        sact(R("AB%d" % h), R("XG%d" % h), F.Abs)
+                        score(h, lambda k: R("AB%d" % h, k, 2048, 16))
+                    pe([(R(cb(h), 256, 384), R("DF", 128 * h, 128 * h + 128), R("IF"), True, True)], 4)
+                if f < 3:
+                    ig = "IG%s%d" % ("ab"[f % 2], h)
+                    nb = "ps%d" % h
+                    for l0 in range(0, 128, CH):
+                        l1 = l0 + CH
+                        sact(R(ig, 16 * l0, 16 * l1), IND("M", 4096, "DL", 128 * h + l0, 128 * h + l1) if f == 0 else IND("M", 4096, "NL%s%d" % ("abc"[f - 1], h), l0, l1), F.Copy)
+                        pe([(R(nb, 320 + l0, 320 + l1), R("LK", 128 * k, 128 * k + 128), R(ig, 16 * l0 + k, 16 * l1, 16), k == 0, k == 15) for k in range(16)])
+                        vcopy(R("NL%s%d" % ("abc"[f], h), l0, l1), R(nb, 320 + l0, 320 + l1))
+                if f > 0:
+                    lw = "LW%s%d" % ("aba"[f - 1], h)
+                    for l0 in range(0, 128, CH):
+                        l1 = l0 + CH
+                        vtt(R(lw, 16 * l0, 16 * l1), IND("X", 4096, "NL%s%d" % ("abc"[f - 1], h), l0, l1), R("QX", 2048 * h + 16 * l0, 2048 * h + 16 * l1), A.is_lt)
+                    pe([(R(cb(h), 384 + k, 512, 16), R(lw, k, 2048, 16), R("G8"), True, True) for k in range(16)])
+                    if f == 1:
+                        sact(R("M1%d" % h), R(cb(h), 384, 512), F.Copy)
+                    if f == 2:
+                        vtt(R("M2%d" % h), R(cb(h), 384, 512), R("M1%d" % h), A.max)
+        for h in range(2):
+            a, b = 128 * h, 128 * h + 128
+            H = str(h)
+            HUE[0] = h
+            s1, at, mb = R(cb(h), 0, 128), R(cb(h), 128, 256), "ps%d" % h
+            vtt(R("M3" + H), R(cb(h), 384, 512), R("M2" + H), A.max)
+            vts(R("CL" + H), R("M3" + H), 8.5, None, A.is_ge)
+            vtt(R("UU" + H), R("CL" + H), at, A.mult)
+            vtt(R("KEY" + H), R("UU" + H), s1, A.max)
+            vscan(R("SCN" + H), R("DMIN"), R("KEY" + H), A.max, A.min)
+            bundle("v", [i_ts(R("OHT" + H, k, k + 16), R("KEY" + H, k, k + 16), R("SCN" + H, k + 15, k + 16), None, A.is_equal) for k in range(0, 128, 16)])
+            vtt(R("W2" + H), R("OHT" + H), R(cb(h), 256, 384), A.mult)
+            vscan(R("ASU" + H), R("DS"), R("W2" + H), A.mult, A.add)
+            bundle("v", [i_ts(R("AM" + H, k, k + 16), R("MK", 0, 16), R("ASU" + H, k + 15, k + 16), None, A.mult) for k in range(0, 128, 16)])
+            pe([(R(mb, 256, 264), R("AM" + H), R("R8"), True, True)], 4)
+            vts(R("AL0" + H), R(mb, 256, 264), -1.0, None, A.add)
+            vts(R("HD" + H, 3, 32, 4), R(mb, 256, 264), R("INV"), None, A.mult)
+            vts(R("NB", 8 * h, 8 * h + 8), R("SCN" + H, 15, 128, 16), BIG, None, A.is_ge)
+            pe([(R(mb, 0, 128), R("OHT" + H), R("I16"), True, True)])
+            sact(R(mb, 128, 256), R(mb, 0, 128), F.Identity, bias=1.0, scale=-1.0)
+            vtt(R("ND", a, b), R("DF", a, b), R(mb, 128, 256), A.mult)
+            if h == 1:
+                pe([(R(mb, 304, 320), R("ONES"), R("NB"), True, True)])
+                node("v", [lambda: V.tensor_reduce(ap(R("NR")), ap(R("ps1", 304, 320)), X, A.add)], [R("ps1", 304, 320)], [R("NR")], 64 * CY)
+                vcopy(R("NRi"), R("NR"))
+                vts(R("NA"), R("NRi"), 255, None, A.bitwise_and)
+                vts(R("AH"), R("NA"), -0.5, None, A.add)
+                vts(R("ZI"), R(Q), R("AH"), 0.5, A.add, A.mult)
+                vcopy(R("ZB", 256 * t, 256 * t + 256), R("ZI"))
+                send("z", "ZB", 256 * t, 256 * t + 256, "RZ", t)
+            for s in range(1, 4):
+                prev = "AL%d%s" % (s - 1, H)
+                sact(R("WM%d" % s + H), IND("PV1", 4096, prev), F.Copy)
+                own(R("WS%d" % s + H), R("WM%d" % s + H))
+                vts(R("AL%d" % s + H), R("WS%d" % s + H, 15, 128, 16), R("SC1"), -1.0, A.mult, A.add)
+                vtt(R("LQ" + H, 128 * s - 128, 128 * s), IND("X", 4096, "AL%d" % s + H), R(Q, a, b), A.is_lt)
+            vtt(R("HD" + H, 2, 32, 4), R("WS1" + H, 15, 128, 16), R("HD" + H, 3, 32, 4), A.subtract)
+            vtt(R("HD" + H, 1, 32, 4), R("WS2" + H, 15, 128, 16), R("WS1" + H, 15, 128, 16), A.subtract)
+            vtt(R("HD" + H, 0, 32, 4), R("WS3" + H, 15, 128, 16), R("WS2" + H, 15, 128, 16), A.subtract)
+            pe([(R(mb, 272, 296), R("LB", 128 * k, 128 * k + 128), R("LQ" + H, k, 384, 16), k == 0, k == 15) for k in range(16)])
+            bundle("v", [i_ts(R("HG" + H, 4 - s, 32, 4), R(mb, 264 + 8 * s, 272 + 8 * s), 8.5, None, A.is_lt) for s in range(1, 4)])
+            vscan(R("HS" + H), R("HG" + H), R("HD" + H), A.mult, A.add)
+            vts(R("AL", 8 * h, 8 * h + 8), R("HS" + H, 3, 32, 4), R("SC1"), -1.0, A.mult, A.add)
+            vts(R("HU", 8 * h, 8 * h + 8), R("HS" + H, 3, 32, 4), R("SC1"), None, A.mult)
+            al = (8 * h, 8 * h + 8)
+            sact(R("WB", 256 * t + a, 256 * t + b), IND("RC1", 4096, "AL", *al), F.Copy)
+            send("ab"[h], "WB", 256 * t + a, 256 * t + b, "RV", t)
+            sact(R("NAT", a, b), IND("IO1", 4096, "AL", *al), F.Copy)
+            vcopy(R("A16", a, b), R("NAT", a, b))
+            sact(R("N4A", a, b), R("NAT", a, b), F.Copy, scale=4096.0)
+            own(R("A1S", a, b), R("NAT", a, b))
+            vtt(R("UT", a, b), R("NAT", a, b), R(mb, 0, 128), A.mult)
+            vtt(R("XS", a, b), IND("X", 4096, "AL", *al), R(Q, a, b), A.add)
+            vts(R("XN", a, b), R("XS", a, b), 0.5, 0.25, A.mult, A.add)
+            if t < RO - 1:
+                sact(R("NP", a, b), IND("M", 4096, "AL", *al), F.Copy)
+                pe([(R("ps%d" % h, 448, 456), R("LK", 128 * k, 128 * k + 128), R("NP", a + k, b, 16), k == 0, k == 15) for k in range(16)])
+                vcopy(R("NLA", *al), R("ps%d" % h, 448, 456))
+                sact(R("NNP", a, b), IND("M", 4096, "NLA", *al), F.Copy)
+            dedupe("A16", lambda m: R("HU", m, m + 1), "EDA" + H, "EQA" + H, "ps7", 0, h, R("N4A", a, b), R("A1S", a, b))
+            target(8 * h, 8 * h + 8, "ps7", 0, "WCA", "TA1", "TA2", "TA3", lambda c0, c1: R("HU", c0, c1), "DWA", "ADR")
+        HUE[0] = 2
+        if t < RO - 1:
+            vcopy(IND("M", 4352, "ADR"), R("NNP"))
+        vcopy(IND("X", 4352, "ADR"), R("XN"))
+        vtt(IND("U", 1280, VA), R("ND"), R("UT"), A.add)
+    dma("y", [(lambda: T.yx[:, :], lambda: ap(R("X", 0, 4096)))], [R("X", 0, 4096)], [], 1048576)
+    vts(R("U", 0, 512), R("U", 0, 512), -1.0, None, A.add)
+    sact(R("U", 512, 1024), R("U", 512, 1024), F.Identity, bias=-1.0)
+    dma("y", [(lambda: T.yu[:, :], lambda: ap(R("U", 0, 1024)))], [R("U", 0, 1024)], [], 524288)
+    o = 256 * (RO - 1)
+    bundle("v", [i_ts(R("YV", 0, 256, 2), R("WB", o, o + 256, 2), -1.0, None, A.add), i_ts(R("YV", 1, 256, 2), R("RV", o + 1, o + 256, 2), -1.0, None, A.add)])
+    Q = "Q%d" % (RO % 2)
+    bundle("v", [i_copy(R(Q, 0, 256, 2), R("ZB", o, o + 256, 2)), i_copy(R(Q, 1, 256, 2), R("RZ", o + 1, o + 256, 2))])
+    py, oy = POOL["YV"]
+    dma("y", [(lambda: T.yv[:, :], lambda: T[py][0:128:16, oy:oy + 256])], [R("YV")], [], 8192)
+    dma("y", [(lambda: T.yq[:, :], lambda: ap(R(Q)))], [R(Q)], [], 65536)
+
+    emit(g, T, nodes)
+
+
+def schedule(nodes, hint):
+    N = len(nodes)
+    succ = [[] for _ in nodes]
+    for i, n in enumerate(nodes):
+        for j in n["need"] | n["order"]:
+            succ[j].append(i)
+    prio = [0.0] * N
+    for i in range(N - 1, -1, -1):
+        n = nodes[i]
+        prio[i] = n["cost"] + n["lat"] + HOP + max([prio[k] for k in succ[i]] + [0.0])
+    prio = [p + hint.get(n["lab"][1], 0.0) + hint.get(n["lab"], 0.0) for p, n in zip(prio, nodes)]
+    left = [len(n["need"] | n["order"]) for n in nodes]
+    ready = [0.0] * N
+    avail = {}
+    free = {}
+    for i, n in enumerate(nodes):
+        if not left[i]:
+            avail.setdefault(n["q"], []).append(i)
+    order = []
+    while len(order) < N:
+        best = None
+        for q, L in avail.items():
+            if not L:
+                continue
+            f = 0.0 if q == "net" else free.get(q, 0.0)
+            s = max(f, min(ready[i] for i in L))
+            c = max((i for i in L if ready[i] <= s), key=lambda i: prio[i])
+            if best is None or s < best[0]:
+                best = (s, q, c)
+        s, q, c = best
+        avail[q].remove(c)
+        n = nodes[c]
+        free[q] = s + n["cost"]
+        e = s + n["cost"] + n["lat"]
+        order.append(c)
+        for k in succ[c]:
+            left[k] -= 1
+            ready[k] = max(ready[k], e + (HOP if c in nodes[k]["need"] else 0.0))
+            if not left[k]:
+                avail.setdefault(nodes[k]["q"], []).append(k)
+    return order, max(free.values())
+
+
+def emit(g, T, nodes):
+    order, _ = schedule(nodes, HINT)
+    eng = {"v": g.vector, "s": g.scalar, "t": g.tensor, "g": g, "y": g.sync}
+    count, known, after, tok = {}, {q: {} for q in eng}, {}, {}
+    sent = 0
+
+    def wait(q, k, v):
+        eng[q].wait_ge(T.sem[k], v)
+        known[q][k] = v
+    for i in order:
+        n = nodes[i]
+        q = n["q"]
+        if q == "net":
+            tok[i] = (n["rsem"], n["tot"])
+            after[i] = {n["rsem"]: n["tot"]}
+            continue
+        K = known[q]
+        ds = [d for d in n["need"] if "remote" not in nodes[d]]
+        todo = {}
+        for d in ds:
+            k, v = tok[d]
+            if K.get(k, 0) < v and todo.get(k, (0, 0))[0] < v:
+                todo[k] = (v, d)
+        for k in list(todo):
+            v, d = todo[k]
+            if any(k2 != k and after[d2].get(k, 0) >= v for k2, (v2, d2) in todo.items()):
+                del todo[k]
+        for k, (v, d) in sorted(todo.items()):
+            wait(q, k, v)
+        for k, (v, d) in todo.items():
+            for k2, v2 in after[d].items():
+                K[k2] = max(K.get(k2, 0), v2)
+        if "remote" in n:
+            n["calls"][0]()
+            sent += n["remote"]
+        elif "dsem" in n:
+            for c in n["calls"]:
+                c().then_inc(T.sem[n["dsem"]], 16)
+            tok[i] = (n["dsem"], n["tot"])
+            after[i] = dict(K)
+            after[i][n["dsem"]] = n["tot"]
+        else:
+            for c in n["calls"]:
+                c().then_inc(T.sem["q" + q], 1)
+            count[q] = count.get(q, 0) + len(n["calls"])
+            tok[i] = ("q" + q, count[q])
+            after[i] = dict(K)
+            after[i]["q" + q] = count[q]
+    for q in "vstg":
+        if known["y"].get("q" + q, 0) < count.get(q, 0):
+            wait("y", "q" + q, count[q])
+    for n in nodes:
+        if "dsem" in n and known["y"].get(n["dsem"], 0) < n["tot"]:
+            wait("y", n["dsem"], n["tot"])
+        if "rsem" in n and known["y"].get(n["rsem"], 0) < n["tot"]:
+            wait("y", n["rsem"], n["tot"])
+    g.wait_ge(T.sem.ls, sent)

@@ -2,6 +2,7 @@ from concourse.mybir import dt, AluOpType, AxisListType, ActivationFunctionType
 
 RO = 3
 BIG = 131072.0
+MAGIC = 8388608.0
 F32, BF, I32, U16 = "float32", "bfloat16", "int32", "uint16"
 SB = {
     "X": (4352, BF), "M": (4352, BF), "U": (1280, F32), "UI": (1024, I32), "PV1": (4096, F32), "RC1": (4096, F32),
@@ -11,9 +12,9 @@ SB = {
     "PI": (1, I32), "PRi": (1, I32), "PGi": (1, I32), "PIf": (1, F32), "PR": (1, F32), "PG": (1, F32), "WT": (1, F32), "WT2": (1, F32),
     "XR": (256, F32), "GR": (128, F32), "CI": (128, F32), "DW0": (16, F32), "DWA": (16, F32), "DWV": (16, F32), "VL0": (16, U16),
     "MK": (128, F32), "MK2": (256, F32), "DX1": (256, F32), "DX2": (256, F32), "DX": (256, F32), "P3": (1, F32), "P4": (1, F32), "SC1": (1, F32), "SC8": (1, F32), "INV": (1, F32),
-    "BQ": (128, BF), "N4V": (256, F32), "N4A": (256, F32), "VU": (16, F32), "HU": (16, F32), "BO": (128, BF), "BW": (128, BF), "LK": (2048, BF), "LB": (2048, BF), "I16": (128, BF), "NI": (128, BF), "IF": (128, F32),
+    "BOF": (128, F32), "BQ": (128, BF), "N4V": (256, F32), "N4A": (256, F32), "VU": (16, F32), "HU": (16, F32), "BO": (128, BF), "BW": (128, BF), "LK": (2048, BF), "LB": (2048, BF), "I16": (128, BF), "NI": (128, BF), "IF": (128, F32),
     "G8": (8, BF), "G8S": (8, BF), "R8": (8, F32), "N8S": (8, BF), "KC1": (128, BF), "KC2": (128, BF), "P0": (1, F32), "P1": (1, F32), "P2": (1, F32), "NAT": (256, F32), "DS": (128, F32), "DMIN": (128, F32), "ONES": (128, BF),
-    "AW": (16, F32), "NB": (16, BF), "NR": (1, F32), "NRi": (1, I32), "NA": (1, I32), "AH": (1, F32), "ZI": (256, I32),
+    "AW": (16, F32), "NB": (16, BF), "NR": (1, F32), "NRi": (1, I32), "NA": (1, I32), "AH": (1, F32), "ZI": (256, F32),
     "DL": (256, U16), "DF": (256, F32), "QX": (4096, BF), "VN": (256, F32), "VM": (256, F32), "VS": (256, F32), "V16": (256, U16), "VL": (16, U16),
     "VA": (16, U16), "CMV": (256, F32), "WCV": (256, F32), "TV1": (16, F32), "TV2": (16, F32), "TV3": (16, F32), "EQV": (2048, BF), "EDV": (128, BF),
     "CMA": (256, F32), "WCA": (256, F32), "TA1": (16, F32), "TA2": (16, F32), "TA3": (16, F32), "ADR": (16, U16),
@@ -22,7 +23,7 @@ SB = {
 }
 for _h in range(2):
     for _n, _v in {"XG": (2048, BF), "AB": (2048, BF), "IGa": (2048, BF), "IGb": (2048, BF), "NLa": (128, U16), "NLb": (128, U16), "NLc": (128, U16),
-                   "LWa": (2048, BF), "LWb": (2048, BF), "M1": (128, F32), "M2": (128, F32), "M3": (128, F32), "CL": (128, F32), "S1": (128, F32), "AT": (128, F32), "UU": (128, F32), "KEY": (128, F32), "SCN": (128, F32), "W2": (128, F32), "ASU": (128, F32),
+                   "LWa": (2048, BF), "LWb": (2048, BF), "M1": (128, BF), "M2": (128, BF), "M3": (128, BF), "CL": (128, BF), "UD": (128, F32), "WS0": (128, F32), "S1": (128, F32), "AT": (128, F32), "UU": (128, F32), "KEY": (128, F32), "SCN": (128, F32), "W2": (128, F32), "ASU": (128, F32),
                    "OHT": (128, BF), "OHS": (128, F32), "NOH": (128, F32), "DT": (128, F32), "AM": (128, F32), "AL0": (8, U16), "AL1": (8, U16), "AL2": (8, U16), "AL3": (8, U16),
                    "WM1": (128, F32), "WM2": (128, F32), "WM3": (128, F32), "WS1": (128, F32), "WS2": (128, F32), "WS3": (128, F32), "LQ": (384, BF),
                    "HG": (32, F32), "HD": (32, F32), "HS": (32, F32), "EQA": (2048, BF), "EDA": (128, BF)}.items():
@@ -34,7 +35,7 @@ SB["RV"] = (256 * RO, F32)
 SB["ZB"] = (256 * RO, BF)
 SB["RZ"] = (256 * RO, BF)
 POOL, SIZE = {}, {}
-SAME = {"XN": "nxh", "ZI": "nxl", "WCV": "pvf", "N4V": "rcf", "N4A": "DX1", "VS": "DX2", "VN": "MK2", "NP": "nhb", "NNP": "nlb", "EQV": "EQA0"}
+SAME = {"WCV": "pvf", "N4V": "rcf", "N4A": "DX1", "VS": "DX2", "VN": "MK2", "NP": "nhb", "NNP": "nlb", "EQV": "EQA0"}
 for _n, (_c, _d) in sorted(SB.items(), key=lambda e: e[0] in SAME):
     if _n in ("WB", "RV", "ZB", "RZ"):
         continue
@@ -55,9 +56,15 @@ BYTES = {F32: 4, I32: 4, BF: 2, U16: 2}
 GC, SCC, CY = 1.5, 3.6, 0.83 * 1.2
 HOP = 70.0
 SMODE = ("v", "v")
-HINT = {"0": 15000.0}
-QXS = "vss"
-XLATE = True
+HINT = {
+    "0": 11600, "v2EDV": 4500, "v1EQA1": -95200, "v1HD1": -64400, "y2Q0": 59300, "v0AL00": 6000, "v1VU": -10100, "v1NA": -7600, "t1ps1": 18400, "v0M30": 3600,
+    "s1IGb1": 4500, "s0XS": -2600, "v0UU0": 49400, "v1NRi": 25400, "v2MK2": -12500, "s1WB": -300, "v0ps3": -13500, "v2PRi": 30900, "v2DMIN": -16600,
+    "v2ONES": -6000, "v2BOF": -19400, "v2DWA": 18900, "s0IGb0": 32100, "v0KEY0": -20600, "v0VL": 21400, "v0ND": 2900, "v1M21": 26600, "t0ps0": 23400,
+    "v0SCN0": -11100, "s0VN": 6000, "v1LWa1": -6700, "v2P3": -29200, "v2BQ": -24200, "2": -12300, "v1AL21": -30600, "v0M20": -11800, "t0ps4": -31100,
+    "v2DX": -21100, "s0NAT": 24000,
+}
+QXS = "sss"
+XLATE = False
 CH = 64
 
 
@@ -186,7 +193,11 @@ def rank_program(g, core, T, topo):
     def i_act(o, i, f, bias=0.0, scale=1.0):
         n = cnt(o)
         c = 65 + n * GC * CY if i[0] == "ind" else max(64, n) * CY
-        return (lambda: Sc.activation(ap(o), ap(i), f, bias=bias, scale=scale), [i], [o], c)
+        cols = [x for x in (bias, scale) if isinstance(x, tuple)]
+
+        def call():
+            return Sc.activation(ap(o), ap(i), f, bias=ap(bias) if isinstance(bias, tuple) else bias, scale=ap(scale) if isinstance(scale, tuple) else scale)
+        return (call, [i] + cols, [o], c)
 
     def sact(o, i, f, bias=0.0, scale=1.0):
         return bundle("s", [i_act(o, i, f, bias, scale)])
@@ -221,10 +232,10 @@ def rank_program(g, core, T, topo):
     pm, om = POOL["M"]
     i = dma("y", [(lambda: T[pm][0:128:16, om:om + 4096], lambda: ap(R("nhb"))), (lambda: T[pm][1:128:16, om:om + 4096], lambda: ap(R("nlb")))],
             [R("nhb"), R("nlb")], [R("M", 0, 4096)], 131072)
-    j = i if XLATE else None
-    j = dma("y", [(lambda: ap(R("X", 0, 4096)), lambda: T.xd[:, :])], [], [R("X", 0, 4096)], 1048576, j)
+    j = dma("y", [(lambda: ap(R("X", 0, 4096)), lambda: T.xd[:, :])], [], [R("X", 0, 4096)], 1048576, i if XLATE else None)
     dma("y", [(lambda: ap(R("pvd")), lambda: T.pv[:, :])], [], [R("pvd")], 131072, j)
-    j = dma("y", [(lambda: ap(R("rcd")), lambda: T.rc[:, :])], [], [R("rcd")], 131072, j)
+    dma("y", [(lambda: ap(R("rcd")), lambda: T.rc[:, :])], [], [R("rcd")], 131072, j)
+    j = i
     iota(R("PI"), [[0, 1]], 0, 1)
     iota(R("PIf"), [[0, 1]], 0, 1)
     iota(R("GR"), [[1, 8], [0, 16]], 0, 0)
@@ -236,19 +247,15 @@ def rank_program(g, core, T, topo):
     bundle("v", [i_copy(R("PR"), R("PRi")), i_copy(R("PG"), R("PGi"))])
     bundle("v", [i_ts(R("WT"), R("PR"), 0.0, 16.0, A.is_equal, A.mult), i_ts(R("WT2"), R("PR"), 1.0, None, A.is_equal)])
     vtt(R("WT"), R("WT"), R("WT2"), A.add)
-    vts(R("BW"), R("GR"), R("PG"), R("WT"), A.is_equal, A.mult)
-    vset(R("LK"), 0.0)
-    bundle("v", [i_copy(R("LK", 128 * k + k, 128 * k + 128, 16), R("BW", k, 128, 16)) for k in range(16)])
     vts(R("BO"), R("GR"), R("PG"), None, A.is_equal)
     vset(R("LB"), 0.0)
     bundle("v", [i_copy(R("LB", 128 * k + k, 128 * k + 128, 16), R("BO", k, 128, 16)) for k in range(16)])
+    sact(R("LK"), R("LB"), F.Identity, scale=R("WT"))
     vts(R("I16"), R("CI"), R("PIf"), None, A.is_equal)
     vts(R("NI"), R("CI"), R("PIf"), -1.0, A.is_equal, A.mult)
-    vts(R("IF"), R("CI"), R("PIf"), None, A.is_equal)
     vts(R("G8"), R("CI", 0, 8), R("PG"), None, A.is_equal)
     vts(R("G8S"), R("CI", 0, 8), R("PG"), 16.0, A.is_equal, A.mult)
-    vts(R("R8"), R("CI", 0, 8), R("PG"), None, A.is_equal)
-    vts(R("MK"), R("XR", 0, 128), R("PR"), None, A.is_equal)
+    vts(R("BOF"), R("GR"), R("PG"), None, A.is_equal)
     bundle("v", [i_ts(R("P0"), R("PIf"), 0.0, None, A.is_equal), i_ts(R("P1"), R("PIf"), 1.0, BIG, A.is_equal, A.mult), i_ts(R("P2"), R("PIf"), 2.0, 65280.0, A.is_equal, A.mult)])
     vtt(R("P1"), R("P1"), R("P2"), A.add)
     vts(R("KC1"), R("XR", 0, 128), R("P0"), None, A.mult)
@@ -257,8 +264,8 @@ def rank_program(g, core, T, topo):
     vts(R("MK2"), R("XR"), R("PR"), None, A.subtract)
     bundle("v", [i_ts(R("DX1"), R("MK2"), 1.0, 4095.0, A.is_equal, A.mult), i_ts(R("DX2"), R("MK2"), 1.0, None, A.is_ge)])
     vtt(R("DX"), R("DX1"), R("DX2"), A.add)
-    bundle("v", [i_ts(R("P3"), R("PR"), 15.0, 1.0 - 1.0 / 4096, A.is_equal, A.mult), i_ts(R("P4"), R("PR"), 15.0, 4095.0, A.is_lt, A.mult)])
-    bundle("v", [i_ts(R("SC1"), R("P3"), 1.0 / 4096, None, A.add), i_ts(R("INV"), R("P4"), 1.0, None, A.add), i_ts(R("SC8"), R("P3"), 1.0 / 4096, 8192.0, A.add, A.mult)])
+    vts(R("P3"), R("PR"), 15.0, 1.0 - 1.0 / 4096, A.is_equal, A.mult)
+    bundle("v", [i_ts(R("SC1"), R("P3"), 1.0 / 4096, None, A.add), i_ts(R("SC8"), R("P3"), 1.0 / 4096, 8192.0, A.add, A.mult)])
     vts(R("BQ"), R("GR"), R("PG"), 0.0625, A.is_equal, A.mult)
     vts(R("DS"), R("XR", 0, 128), 0.0, None, A.not_equal)
     vts(R("DMIN"), R("DS"), -1048576.0, 1048575.0, A.mult, A.add)
@@ -308,7 +315,8 @@ def rank_program(g, core, T, topo):
 
     def target(c0, c1, bank, base, wc, t1, t2, t3, aw, dw, out):
         l0, l1 = 16 * c0, 16 * c1
-        own(R(wc, l0, l1), R(bank, base + l0, base + l1))
+        for l in range(l0, l1, 128):
+            own(R(wc, l, l + 128), R(bank, base + l, base + l + 128))
         vts(R(t1, c0, c1), R(wc, l0 + 15, l1, 16), R("SC8"), -8192.0, A.mult, A.add)
         vtt(R(t2, c0, c1), R(t1, c0, c1), R(dw, c0, c1), A.min)
         vtt(R(t3, c0, c1), R(t2, c0, c1), aw(c0, c1), A.max)
@@ -338,9 +346,9 @@ def rank_program(g, core, T, topo):
                 a, b = 128 * h, 128 * h + 128
                 HUE[0] = h
                 bundle("s", [i_act(R("VN", a, b, 2), R("WB", o + a, o + b, 2), F.Copy), i_act(R("VN", a + 1, b, 2), R("RV", o + a + 1, o + b, 2), F.Copy)])
-                own(R("VS", a, b), R("VN", a, b))
-                vts(R("VL", 8 * h, 8 * h + 8), R("VS", a + 15, b, 16), R("SC1"), -1.0, A.mult, A.add)
-                vts(R("VU", 8 * h, 8 * h + 8), R("VS", a + 15, b, 16), R("SC1"), None, A.mult)
+                own(R("ps3", 256 + a, 256 + b), R("VN", a, b))
+                vts(R("VL", 8 * h, 8 * h + 8), R("ps3", 256 + a + 15, 256 + b, 16), R("SC1"), -1.0, A.mult, A.add)
+                vts(R("VU", 8 * h, 8 * h + 8), R("ps3", 256 + a + 15, 256 + b, 16), R("SC1"), None, A.mult)
                 vts(R("DL", a, b), IND("U", 1024, "VL", 8 * h, 8 * h + 8), -1.0, None, A.add)
                 sact(R("DF", a, b), IND("U", 1024, "VL", 8 * h, 8 * h + 8), F.Copy)
             for h in range(2):
@@ -359,7 +367,7 @@ def rank_program(g, core, T, topo):
                 a, b = 128 * h, 128 * h + 128
                 sact(R("N4V", a, b), R("VN", a, b), F.Copy, scale=4096.0)
                 vcopy(R("V16", a, b), R("VN", a, b))
-                dedupe("V16", lambda m: R("VU", m, m + 1), "EDV", "EQV", "ps7", 256, h, R("N4V", a, b), R("VS", a, b))
+                dedupe("V16", lambda m: R("VU", m, m + 1), "EDV", "EQV", "ps7", 256, h, R("N4V", a, b), R("ps3", 256 + a, 256 + b))
             target(0, 16, "ps7", 256, "WCV", "TV1", "TV2", "TV3", lambda c0, c1: R("VU", c0, c1), "DWV", "VA")
         cb = lambda h: "ps%d" % (4 + h)
 
@@ -377,7 +385,7 @@ def rank_program(g, core, T, topo):
                     if SMODE[h] == "s":
                         sact(R("XG%d" % h), d, F.Copy)
                         for c in range(4):
-                            bk = ("ps2", "ps3", "ps6")[turn[0] % 3]
+                            bk = ("ps2", "ps6")[turn[0] % 2]
                             turn[0] += 1
                             mm = []
                             for kk in range(4):
@@ -390,7 +398,6 @@ def rank_program(g, core, T, topo):
                         vtt(R("XG%d" % h), d, R("QX", 2048 * h, 2048 * h + 2048), A.subtract)
                         sact(R("AB%d" % h), R("XG%d" % h), F.Abs)
                         score(h, lambda k: R("AB%d" % h, k, 2048, 16))
-                    pe([(R(cb(h), 256, 384), R("DF", 128 * h, 128 * h + 128), R("IF"), True, True)], 4)
                 if f < 3:
                     ig = "IG%s%d" % ("ab"[f % 2], h)
                     nb = "ps%d" % h
@@ -420,14 +427,13 @@ def rank_program(g, core, T, topo):
             vtt(R("KEY" + H), R("UU" + H), s1, A.max)
             vscan(R("SCN" + H), R("DMIN"), R("KEY" + H), A.max, A.min)
             bundle("v", [i_ts(R("OHT" + H, k, k + 16), R("KEY" + H, k, k + 16), R("SCN" + H, k + 15, k + 16), None, A.is_equal) for k in range(0, 128, 16)])
-            vtt(R("W2" + H), R("OHT" + H), R(cb(h), 256, 384), A.mult)
-            vscan(R("ASU" + H), R("DS"), R("W2" + H), A.mult, A.add)
-            bundle("v", [i_ts(R("AM" + H, k, k + 16), R("MK", 0, 16), R("ASU" + H, k + 15, k + 16), None, A.mult) for k in range(0, 128, 16)])
-            pe([(R(mb, 256, 264), R("AM" + H), R("R8"), True, True)], 4)
-            vts(R("AL0" + H), R(mb, 256, 264), -1.0, None, A.add)
-            vts(R("HD" + H, 3, 32, 4), R(mb, 256, 264), R("INV"), None, A.mult)
-            vts(R("NB", 8 * h, 8 * h + 8), R("SCN" + H, 15, 128, 16), BIG, None, A.is_ge)
             pe([(R(mb, 0, 128), R("OHT" + H), R("I16"), True, True)])
+            vtt(R("UD" + H), R("DF", a, b), R(mb, 0, 128), A.mult)
+            pe([(R(mb, 320, 448), R("BOF"), R("UD" + H), True, True)], 4)
+            own(R("WS0" + H), R(mb, 320, 448))
+            vts(R("AL0" + H), R("WS0" + H, 15, 128, 16), R("SC1"), -1.0, A.mult, A.add)
+            vcopy(R("HD" + H, 3, 32, 4), R("WS0" + H, 15, 128, 16))
+            vts(R("NB", 8 * h, 8 * h + 8), R("SCN" + H, 15, 128, 16), BIG, None, A.is_ge)
             sact(R(mb, 128, 256), R(mb, 0, 128), F.Identity, bias=1.0, scale=-1.0)
             vtt(R("ND", a, b), R("DF", a, b), R(mb, 128, 256), A.mult)
             if h == 1:
@@ -435,9 +441,10 @@ def rank_program(g, core, T, topo):
                 node("v", [lambda: V.tensor_reduce(ap(R("NR")), ap(R("ps1", 304, 320)), X, A.add)], [R("ps1", 304, 320)], [R("NR")], 64 * CY)
                 vcopy(R("NRi"), R("NR"))
                 vts(R("NA"), R("NRi"), 255, None, A.bitwise_and)
-                vts(R("AH"), R("NA"), -0.5, None, A.add)
-                vts(R("ZI"), R(Q), R("AH"), 0.5, A.add, A.mult)
-                vcopy(R("ZB", 256 * t, 256 * t + 256), R("ZI"))
+                vts(R("AH"), R("NA"), 0.5, -0.25, A.mult, A.add)
+                sact(R("ZI"), R(Q), F.Identity, bias=R("AH"), scale=0.5)
+                sact(R("ZI"), R("ZI"), F.Identity, bias=MAGIC)
+                sact(R("ZB", 256 * t, 256 * t + 256), R("ZI"), F.Identity, bias=-MAGIC)
                 send("z", "ZB", 256 * t, 256 * t + 256, "RZ", t)
             for s in range(1, 4):
                 prev = "AL%d%s" % (s - 1, H)
@@ -459,21 +466,23 @@ def rank_program(g, core, T, topo):
             sact(R("NAT", a, b), IND("IO1", 4096, "AL", *al), F.Copy)
             vcopy(R("A16", a, b), R("NAT", a, b))
             sact(R("N4A", a, b), R("NAT", a, b), F.Copy, scale=4096.0)
-            own(R("A1S", a, b), R("NAT", a, b))
+            own(R("ps3", a, b), R("NAT", a, b))
             vtt(R("UT", a, b), R("NAT", a, b), R(mb, 0, 128), A.mult)
             vtt(R("XS", a, b), IND("X", 4096, "AL", *al), R(Q, a, b), A.add)
-            vts(R("XN", a, b), R("XS", a, b), 0.5, 0.25, A.mult, A.add)
+            sact(R("XS", a, b), R("XS", a, b), F.Identity, bias=0.25, scale=0.5)
+            sact(R("XS", a, b), R("XS", a, b), F.Identity, bias=MAGIC)
+            sact(R("XS", a, b), R("XS", a, b), F.Identity, bias=-MAGIC)
             if t < RO - 1:
                 sact(R("NP", a, b), IND("M", 4096, "AL", *al), F.Copy)
                 pe([(R("ps%d" % h, 448, 456), R("LK", 128 * k, 128 * k + 128), R("NP", a + k, b, 16), k == 0, k == 15) for k in range(16)])
                 vcopy(R("NLA", *al), R("ps%d" % h, 448, 456))
                 sact(R("NNP", a, b), IND("M", 4096, "NLA", *al), F.Copy)
-            dedupe("A16", lambda m: R("HU", m, m + 1), "EDA" + H, "EQA" + H, "ps7", 0, h, R("N4A", a, b), R("A1S", a, b))
-            target(8 * h, 8 * h + 8, "ps7", 0, "WCA", "TA1", "TA2", "TA3", lambda c0, c1: R("HU", c0, c1), "DWA", "ADR")
+            dedupe("A16", lambda m: R("HU", m, m + 1), "EDA" + H, "EQA" + H, "ps7", 0, h, R("N4A", a, b), R("ps3", a, b))
+        target(0, 16, "ps7", 0, "WCA", "TA1", "TA2", "TA3", lambda c0, c1: R("HU", c0, c1), "DWA", "ADR")
         HUE[0] = 2
         if t < RO - 1:
             vcopy(IND("M", 4352, "ADR"), R("NNP"))
-        vcopy(IND("X", 4352, "ADR"), R("XN"))
+        vcopy(IND("X", 4352, "ADR"), R("XS"))
         vtt(IND("U", 1280, VA), R("ND"), R("UT"), A.add)
     dma("y", [(lambda: T.yx[:, :], lambda: ap(R("X", 0, 4096)))], [R("X", 0, 4096)], [], 1048576)
     vts(R("U", 0, 512), R("U", 0, 512), -1.0, None, A.add)

from concourse.mybir import dt, AluOpType, AxisListType, ActivationFunctionType

RO = 3
BIG = 131072.0
MAGIC = 8388608.0
F32, BF, I32, U16 = "float32", "bfloat16", "int32", "uint16"
SB = {
    "X": (4352, BF), "M": (4352, BF), "U": (1280, F32), "UI": (1024, I32), "PV1": (4096, F32), "RC1": (4096, F32),
    "IO1": (4096, F32),
    "nxd": (256, I32), "pvd": (256, I32), "rcd": (256, I32), "pvf": (256, F32), "rcf": (256, F32),
    "nxh": (256, I32), "nxl": (256, I32), "nhb": (256, BF), "nlb": (256, BF),
    "PI": (1, I32), "PRi": (1, I32), "PGi": (1, I32), "PIf": (1, F32), "PR": (1, F32), "PG": (1, F32), "WT": (1, F32), "WT2": (1, F32),
    "XR": (256, F32), "GR": (128, F32), "CI": (128, F32), "DW0": (16, F32), "DWA": (16, F32), "DWV": (16, F32), "VL0": (16, U16),
    "MK": (128, F32), "MK2": (256, F32), "DX1": (256, F32), "DX2": (256, F32), "DX": (256, F32), "P3": (1, F32), "P4": (1, F32), "SC1": (1, F32), "SC8": (1, F32), "INV": (1, F32),
    "BOF": (128, F32), "BQ": (128, BF), "N4V": (256, F32), "N4A": (256, F32), "VU": (16, F32), "HU": (16, F32), "BO": (128, BF), "BW": (128, BF), "LK": (2048, BF), "LB": (2048, BF), "I16": (128, BF), "NI": (128, BF), "IF": (128, F32),
    "G8": (8, BF), "G8S": (8, BF), "R8": (8, F32), "N8S": (8, BF), "KC1": (128, BF), "KC2": (128, BF), "P0": (1, F32), "P1": (1, F32), "P2": (1, F32), "NAT": (256, F32), "DS": (128, F32), "DMIN": (128, F32), "ONES": (128, BF),
    "AW": (16, F32), "NB": (16, BF), "NR": (1, F32), "NRi": (1, I32), "NA": (1, I32), "AH": (1, F32), "ZI": (256, F32),
    "DL": (256, U16), "DF": (256, F32), "QX": (4096, BF), "VN": (256, F32), "VM": (256, F32), "VS": (256, F32), "V16": (256, U16), "VL": (16, U16),
    "VA": (16, U16), "CMV": (256, F32), "WCV": (256, F32), "TV1": (16, F32), "TV2": (16, F32), "TV3": (16, F32), "EQV": (2048, BF), "EDV": (128, BF),
    "CMA": (256, F32), "WCA": (256, F32), "TA1": (16, F32), "TA2": (16, F32), "TA3": (16, F32), "ADR": (16, U16),
    "AL": (16, U16), "A16": (256, U16), "A1M": (256, F32), "A1S": (256, F32), "ND": (256, F32), "UV": (256, F32), "UT": (256, F32), "XS": (256, F32), "XN": (256, I32),
    "NP": (256, BF), "NNP": (256, BF), "NLA": (16, U16), "YV": (256, F32),
}
for _h in range(2):
    for _n, _v in {"XG": (2048, BF), "AB": (2048, BF), "IGa": (2048, BF), "IGb": (2048, BF), "NLa": (128, U16), "NLb": (128, U16), "NLc": (128, U16),
                   "LWa": (2048, BF), "LWb": (2048, BF), "M1": (128, BF), "M2": (128, BF), "M3": (128, BF), "CL": (128, BF), "UD": (128, F32), "WS0": (128, F32), "S1": (128, F32), "AT": (128, F32), "UU": (128, F32), "KEY": (128, F32), "SCN": (128, F32), "W2": (128, F32), "ASU": (128, F32),
                   "OHT": (128, BF), "OHS": (128, F32), "NOH": (128, F32), "DT": (128, F32), "AM": (128, F32), "AL0": (8, U16), "AL1": (8, U16), "AL2": (8, U16), "AL3": (8, U16),
                   "WM1": (128, F32), "WM2": (128, F32), "WM3": (128, F32), "WS1": (128, F32), "WS2": (128, F32), "WS3": (128, F32), "LQ": (384, BF),
                   "HG": (32, F32), "HD": (32, F32), "HS": (32, F32), "EQA": (2048, BF), "EDA": (128, BF)}.items():
        SB[_n + str(_h)] = _v
for _t in range(2):
    SB["Q%d" % _t] = (256, BF)
SB["WB"] = (256 * RO, F32)
SB["RV"] = (256 * RO, F32)
SB["ZB"] = (256 * RO, BF)
SB["RZ"] = (256 * RO, BF)
POOL, SIZE = {}, {}
SAME = {"WCV": "pvf", "N4V": "rcf", "N4A": "DX1", "VS": "DX2", "VN": "MK2", "NP": "nhb", "NNP": "nlb", "EQV": "EQA0"}
for _n, (_c, _d) in sorted(SB.items(), key=lambda e: e[0] in SAME):
    if _n in ("WB", "RV", "ZB", "RZ"):
        continue
    if _n in SAME:
        POOL[_n] = POOL[SAME[_n]]
        continue
    _o = SIZE.get(_d, 0)
    POOL[_n] = ("p" + _d, _o)
    SIZE[_d] = _o + (_c + 15) // 16 * 16
SCRATCH = {"p" + _d: ("sbuf", [128, _c], _d) for _d, _c in SIZE.items()}
for _n in ("WB", "RV", "ZB", "RZ"):
    SCRATCH[_n] = ("sbuf", [128, SB[_n][0]], SB[_n][1])
for _i in range(8):
    SCRATCH["ps%d" % _i] = ("psum", [128, 512], F32)
NDMA = 24
SEMAPHORES = ["qv", "qs", "qt", "qg", "ls"] + ["d%d" % i for i in range(NDMA)] + ["r%s%d" % (a, t) for a in "abz" for t in range(RO)]
BYTES = {F32: 4, I32: 4, BF: 2, U16: 2}
GC, SCC, CY = 1.5, 3.6, 0.83 * 1.2
HOP = 70.0
SMODE = ("v", "v")
HINT = {
    "0": 11600, "v2EDV": 4500, "v1EQA1": -95200, "v1HD1": -64400, "y2Q0": 59300, "v0AL00": 6000, "v1VU": -10100, "v1NA": -7600, "t1ps1": 18400, "v0M30": 3600,
    "s1IGb1": 4500, "s0XS": -2600, "v0UU0": 49400, "v1NRi": 25400, "v2MK2": -12500, "s1WB": -300, "v0ps3": -13500, "v2PRi": 30900, "v2DMIN": -16600,
    "v2ONES": -6000, "v2BOF": -19400, "v2DWA": 18900, "s0IGb0": 32100, "v0KEY0": -20600, "v0VL": 21400, "v0ND": 2900, "v1M21": 26600, "t0ps0": 23400,
    "v0SCN0": -11100, "s0VN": 6000, "v1LWa1": -6700, "v2P3": -29200, "v2BQ": -24200, "2": -12300, "v1AL21": -30600, "v0M20": -11800, "t0ps4": -31100,
    "v2DX": -21100, "s0NAT": 24000,
}
QXS = "sss"
XLATE = False
CH = 64


def rank_program(g, core, T, topo):
    rank = T.rank_of(core)
    if rank is None:
        return
    A, F, X = AluOpType, ActivationFunctionType, AxisListType.X
    V, Sc, Te = g.vector, g.scalar, g.tensor
    nodes, acc, ndma, HUE, turn = [], {}, [0], [2], [0]

    def R(n, a=0, b=None, s=1):
        if n in POOL:
            p, o = POOL[n]
            return (p, o + a, o + (SB[n][0] if b is None else b), s, n)
        return (n, a, SCRATCH[n][1][-1] if b is None else b, s, n)

    def IND(n, w, l, c=0, d=None):
        return ("ind", R(n, 0, w), R(l, c, d))

    def ap(r):
        if r[0] == "ind":
            return ap(r[1]).indirect(ap(r[2]))
        t = T[r[0]]
        if len(SCRATCH[r[0]][1]) == 3:
            return t[:, :, r[1]:r[2]]
        return t[:, r[1]:r[2]] if r[3] == 1 else t[:, r[1]:r[2]:r[3]]

    def cnt(r):
        if r[0] == "ind":
            return 16 * (r[2][2] - r[2][1])
        k = (r[2] - r[1] + r[3] - 1) // r[3]
        return k * 8 if len(SCRATCH[r[0]][1]) == 3 else k

    def two(r):
        r = r[1] if r[0] == "ind" else r
        return BYTES[SCRATCH[r[0]][2]] == 2

    def meet(a, b):
        if a[1] >= b[2] or b[1] >= a[2]:
            return False
        return not (a[3] == b[3] and a[3] > 1 and (a[1] - b[1]) % a[3])

    def node(q, calls, reads, writes, cost, lat=0.0, after=(), ahead=(), **kw):
        i = len(nodes)
        need, order = set(after), set(ahead)
        touch = []
        for r in reads:
            touch += [(r[1], False), (r[2], False)] if r[0] == "ind" else [(r, False)]
        for w in writes:
            touch += [(w[1], True), (w[2], False)] if w[0] == "ind" else [(w, True)]
        for r, wr in touch:
            for j, r2, wr2 in acc.setdefault(r[0], []):
                if j == i:
                    continue
                bank = r[0][:2] == "ps" and nodes[j]["q"] != q
                if bank or ((wr or wr2) and meet(r, r2)):
                    if nodes[j]["q"] == q and q == "t" and wr2 and wr:
                        order.add(j)
                    else:
                        need.add(j)
                elif r[0][:2] == "ps" and wr and wr2:
                    order.add(j)
        for r, wr in touch:
            L = acc[r[0]]
            if wr and r[3] == 1:
                L[:] = [e for e in L if not (e[1][1] >= r[1] and e[1][2] <= r[2] and (r[0][:2] != "ps"))]
            if r[0][:2] == "ps" and len(L) > 60:
                del L[:20]
            L.append((i, r, wr))
        nodes.append(dict(q=q, calls=calls, need=need, order=order - need, cost=cost, lat=lat, lab="%s%d%s" % (q, HUE[0], (writes[0][1] if writes[0][0] == "ind" else writes[0])[4] if writes else ""), **kw))
        return i

    def vcost(o, ins, per):
        n = cnt(o)
        if o[0] == "ind":
            return 50 + n * SCC * CY
        for r in ins:
            if r[0] == "ind":
                return 50 + n * GC * CY
        if per == 1 and two(o) and all(two(r) for r in ins):
            per = 0.5
        if per == 2 and any(r[0][:2] == "ps" for r in ins):
            per = 1
        return max(64, n * per) * CY

    def bundle(q, items):
        return node(q, [c for c, _, _, _ in items], [r for _, rs, _, _ in items for r in rs], [w for _, _, ws, _ in items for w in ws],
                    sum(c for _, _, _, c in items))

    def i_copy(o, i):
        return (lambda: V.tensor_copy(ap(o), ap(i)), [i], [o], vcost(o, [i], 1))

    def i_tt(o, a, b, op):
        return (lambda: V.tensor_tensor(ap(o), ap(a), ap(b), op), [a, b], [o], vcost(o, [a, b], 2))

    def i_ts(o, a, s1, s2, op0, op1=None):
        rs = [a] + [s for s in (s1, s2) if isinstance(s, tuple)]

        def call():
            x1 = ap(s1) if isinstance(s1, tuple) else s1
            x2 = ap(s2) if isinstance(s2, tuple) else s2
            if op1 is None:
                return V.tensor_scalar(ap(o), ap(a), x1, None, op0)
            return V.tensor_scalar(ap(o), ap(a), x1, x2, op0, op1)
        return (call, rs, [o], vcost(o, [a], 1))

    def i_set(o, v):
        return (lambda: V.memset(ap(o), v), [], [o], vcost(o, [], 1))

    def vcopy(o, i):
        return bundle("v", [i_copy(o, i)])

    def vtt(o, a, b, op):
        return bundle("v", [i_tt(o, a, b, op)])

    def vts(o, a, s1, s2, op0, op1=None):
        return bundle("v", [i_ts(o, a, s1, s2, op0, op1)])

    def vset(o, v):
        return bundle("v", [i_set(o, v)])

    def vscan(o, d0, d1, op0, op1):
        return node("v", [lambda: V.tensor_tensor_scan(ap(o), ap(d0), ap(d1), 0.0, op0, op1)], [d0, d1], [o], vcost(o, [d0], 1))

    def i_act(o, i, f, bias=0.0, scale=1.0):
        n = cnt(o)
        c = 65 + n * GC * CY if i[0] == "ind" else max(64, n) * CY
        cols = [x for x in (bias, scale) if isinstance(x, tuple)]

        def call():
            return Sc.activation(ap(o), ap(i), f, bias=ap(bias) if isinstance(bias, tuple) else bias, scale=ap(scale) if isinstance(scale, tuple) else scale)
        return (call, [i] + cols, [o], c)

    def sact(o, i, f, bias=0.0, scale=1.0):
        return bundle("s", [i_act(o, i, f, bias, scale)])

    def pe(mms, x4=1):
        def call(m):
            return lambda: Te.matmul(ap(m[0]), ap(m[1]), ap(m[2]), m[3], m[4])
        return node("t", [call(m) for m in mms], [m[k] for m in mms for k in (1, 2)], [m[0] for m in mms],
                    sum(max(64, cnt(m[2])) * x4 * CY for m in mms))

    def dma(q, pairs, reads, writes, nbytes, then=None):
        k = ndma[0]
        ndma[0] += 1
        e = g.sync if q == "y" else Sc

        def call(o, i):
            return lambda: e.dma_start(o(), i())
        return node(q, [call(o, i) for o, i in pairs], reads, writes, 60.0 * len(pairs), 2000.0 + nbytes / 200.0, ahead=() if then is None else (then,), dsem="d%d" % k, tot=16 * len(pairs))

    def iota(o, pat, base, cm):
        n = cnt(o)
        i32 = SCRATCH[o[0]][2] == I32
        return node("g", [(lambda: g.iota(ap(o), pat, base, cm)) if i32 else (lambda: g.iota(ap(o), pat, base, cm, allow_small_or_imprecise_dtypes=True))],
                    [], [o], 130 + n * 2 * CY)

    dma("y", [(lambda: ap(R("nxd")), lambda: T.nx[:, :])], [], [R("nxd")], 131072)
    dma("s", [(lambda: ap(R("UI")), lambda: T.ul[:, :])], [], [R("UI")], 524288)
    dma("y", [(lambda: ap(R("Q0")), lambda: T.mv[:, :])], [], [R("Q0")], 65536)
    vset(R("M", 0, 4096), 0.0)
    bundle("v", [i_ts(R("nxh"), R("nxd"), 4, None, A.arith_shift_right), i_ts(R("nxl"), R("nxd"), 15, None, A.bitwise_and)])
    bundle("v", [i_copy(R("nhb"), R("nxh")), i_copy(R("nlb"), R("nxl"))])
    pm, om = POOL["M"]
    i = dma("y", [(lambda: T[pm][0:128:16, om:om + 4096], lambda: ap(R("nhb"))), (lambda: T[pm][1:128:16, om:om + 4096], lambda: ap(R("nlb")))],
            [R("nhb"), R("nlb")], [R("M", 0, 4096)], 131072)
    j = dma("y", [(lambda: ap(R("X", 0, 4096)), lambda: T.xd[:, :])], [], [R("X", 0, 4096)], 1048576, i if XLATE else None)
    dma("y", [(lambda: ap(R("pvd")), lambda: T.pv[:, :])], [], [R("pvd")], 131072, j)
    dma("y", [(lambda: ap(R("rcd")), lambda: T.rc[:, :])], [], [R("rcd")], 131072, j)
    j = i
    iota(R("PI"), [[0, 1]], 0, 1)
    iota(R("PIf"), [[0, 1]], 0, 1)
    iota(R("GR"), [[1, 8], [0, 16]], 0, 0)
    iota(R("XR"), [[0, 16], [1, 16]], 0, 0)
    iota(R("CI"), [[1, 128]], 0, 0)
    iota(R("DW0"), [[16, 16]], 0, 0)
    iota(R("IO1"), [[1, 4096]], 1, 0)
    bundle("v", [i_ts(R("PRi"), R("PI"), 15, None, A.bitwise_and), i_ts(R("PGi"), R("PI"), 4, None, A.arith_shift_right)])
    bundle("v", [i_copy(R("PR"), R("PRi")), i_copy(R("PG"), R("PGi"))])
    bundle("v", [i_ts(R("WT"), R("PR"), 0.0, 16.0, A.is_equal, A.mult), i_ts(R("WT2"), R("PR"), 1.0, None, A.is_equal)])
    vtt(R("WT"), R("WT"), R("WT2"), A.add)
    vts(R("BO"), R("GR"), R("PG"), None, A.is_equal)
    vset(R("LB"), 0.0)
    bundle("v", [i_copy(R("LB", 128 * k + k, 128 * k + 128, 16), R("BO", k, 128, 16)) for k in range(16)])
    sact(R("LK"), R("LB"), F.Identity, scale=R("WT"))
    vts(R("I16"), R("CI"), R("PIf"), None, A.is_equal)
    vts(R("NI"), R("CI"), R("PIf"), -1.0, A.is_equal, A.mult)
    vts(R("G8"), R("CI", 0, 8), R("PG"), None, A.is_equal)
    vts(R("G8S"), R("CI", 0, 8), R("PG"), 16.0, A.is_equal, A.mult)
    vts(R("BOF"), R("GR"), R("PG"), None, A.is_equal)
    bundle("v", [i_ts(R("P0"), R("PIf"), 0.0, None, A.is_equal), i_ts(R("P1"), R("PIf"), 1.0, BIG, A.is_equal, A.mult), i_ts(R("P2"), R("PIf"), 2.0, 65280.0, A.is_equal, A.mult)])
    vtt(R("P1"), R("P1"), R("P2"), A.add)
    vts(R("KC1"), R("XR", 0, 128), R("P0"), None, A.mult)
    vts(R("KC2"), R("XR", 0, 128), R("P0"), R("P1"), A.mult, A.add)
    vts(R("N8S"), R("CI", 0, 8), R("PG"), -16.0, A.is_equal, A.mult)
    vts(R("MK2"), R("XR"), R("PR"), None, A.subtract)
    bundle("v", [i_ts(R("DX1"), R("MK2"), 1.0, 4095.0, A.is_equal, A.mult), i_ts(R("DX2"), R("MK2"), 1.0, None, A.is_ge)])
    vtt(R("DX"), R("DX1"), R("DX2"), A.add)
    vts(R("P3"), R("PR"), 15.0, 1.0 - 1.0 / 4096, A.is_equal, A.mult)
    bundle("v", [i_ts(R("SC1"), R("P3"), 1.0 / 4096, None, A.add), i_ts(R("SC8"), R("P3"), 1.0 / 4096, 8192.0, A.add, A.mult)])
    vts(R("BQ"), R("GR"), R("PG"), 0.0625, A.is_equal, A.mult)
    vts(R("DS"), R("XR", 0, 128), 0.0, None, A.not_equal)
    vts(R("DMIN"), R("DS"), -1048576.0, 1048575.0, A.mult, A.add)
    vset(R("ONES"), 1.0)
    vts(R("DWA"), R("DW0"), R("PR"), 4097.0, A.add, A.add)
    vts(R("DWV"), R("DW0"), R("PR"), 1025.0, A.add, A.add)
    vts(R("VL0"), R("DW0"), R("PR"), 4.0, A.add, A.mult)
    for h in range(2):
        vset(R("HG%d" % h), 0.0)
    for n, d, f in (("PV1", "pvd", "pvf"), ("RC1", "rcd", "rcf")):
        vts(R(f), R(d), 1.0, None, A.add)
        p, o = POOL[n]

        def dst(p, o, i):
            return lambda: T[p][i:128:16, o:o + 4096]
        dma("y", [(dst(p, o, i), (lambda f: lambda: ap(R(f)))(f)) for i in range(16)], [R(f)], [R(n)], 2097152, j)
    vts(R("U", 0, 1024), R("UI"), 1.0, None, A.add)

    def own(o, i):
        n = cnt(i)
        vscan(o, R("DX", 0, n), i, A.mult, A.max)

    def dedupe(nat16, scal, ed, eq, bank, base, h, natd, pref):
        c0 = 128 * h
        first = []
        ms = list(range(0, 8 * h + 7))
        full = [m for m in ms if m < 8 * h]
        part = [m for m in ms if m >= 8 * h]

        def eqs(l):
            its = []
            for m in l:
                b = max(0, 16 * (m + 1) - c0)
                its.append(i_ts(R(eq, 128 * m + b, 128 * m + 128), R(nat16, c0 + b, c0 + 128), scal(m), None, A.is_equal))
            bundle("v", its)

        def mm(m, st, sp):
            b = max(0, 16 * (m + 1) - c0)
            return (R(bank, base + c0 + b, base + c0 + 128), R("BO"), R(eq, 128 * m + b, 128 * m + 128), st, sp)
        if full:
            eqs(full)
        reg = R(bank, base + c0, base + c0 + 128)
        pe([(reg, R("BQ"), R("ONES"), True, False)] + [mm(m, False, False) for m in full])
        eqs(part)
        vtt(R(ed), natd, pref, A.is_equal)
        pe([(reg, R("BO"), R(ed), False, False)] + [mm(m, False, m == part[-1]) for m in part])

    def target(c0, c1, bank, base, wc, t1, t2, t3, aw, dw, out):
        l0, l1 = 16 * c0, 16 * c1
        for l in range(l0, l1, 128):
            own(R(wc, l, l + 128), R(bank, base + l, base + l + 128))
        vts(R(t1, c0, c1), R(wc, l0 + 15, l1, 16), R("SC8"), -8192.0, A.mult, A.add)
        vtt(R(t2, c0, c1), R(t1, c0, c1), R(dw, c0, c1), A.min)
        vtt(R(t3, c0, c1), R(t2, c0, c1), aw(c0, c1), A.max)
        vts(R(out, c0, c1), R(t3, c0, c1), -1.0, None, A.add)

    recv = {}

    def send(name, buf, a, b, rbuf, t):
        dst = T.cores[(rank + 1 + t % 3) % 4]
        rid, pid = topo.addr(dst)[0:2]
        src = T.cores[(rank - 1 - t % 3) % 4]
        i = node("g", [lambda: g.remote_dma(T[rbuf][:, a:b], T[buf][:, a:b], T.sem["r%s%d" % (name, t)], T.sem.ls, pid=pid, routing_id=rid, dma_engine_mask=topo.mask(core, dst))],
                 [R(buf, a, b)], [], 900.0, remote=len(topo.engines(core, dst)))
        recv[name, t] = node("net", [], [], [R(rbuf, a, b)], 0.0, 3500.0, after=(i,), rsem="r%s%d" % (name, t), tot=len(topo.engines(src, core)))

    for t in range(RO):
        Q, QP = "Q%d" % (t % 2), "Q%d" % ((t + 1) % 2)
        o = 256 * (t - 1)
        if t == 0:
            for h in range(2):
                vcopy(R("DL", 128 * h, 128 * h + 128), R("UI", 512 * h, 512 * h + 512, 4))
                vts(R("DF", 128 * h, 128 * h + 128), R("UI", 512 * h, 512 * h + 512, 4), 1.0, None, A.add)
            VA = "VL0"
        else:
            VA = "VA"
            for h in range(2):
                a, b = 128 * h, 128 * h + 128
                HUE[0] = h
                bundle("s", [i_act(R("VN", a, b, 2), R("WB", o + a, o + b, 2), F.Copy), i_act(R("VN", a + 1, b, 2), R("RV", o + a + 1, o + b, 2), F.Copy)])
                own(R("ps3", 256 + a, 256 + b), R("VN", a, b))
                vts(R("VL", 8 * h, 8 * h + 8), R("ps3", 256 + a + 15, 256 + b, 16), R("SC1"), -1.0, A.mult, A.add)
                vts(R("VU", 8 * h, 8 * h + 8), R("ps3", 256 + a + 15, 256 + b, 16), R("SC1"), None, A.mult)
                vts(R("DL", a, b), IND("U", 1024, "VL", 8 * h, 8 * h + 8), -1.0, None, A.add)
                sact(R("DF", a, b), IND("U", 1024, "VL", 8 * h, 8 * h + 8), F.Copy)
            for h in range(2):
                a, b = 128 * h, 128 * h + 128
                HUE[0] = h
                bundle("s", [i_act(R(Q, a, b, 2), R("ZB", o + a, o + b, 2), F.Copy), i_act(R(Q, a + 1, b, 2), R("RZ", o + a + 1, o + b, 2), F.Copy)])
        for h in range(2):
            HUE[0] = h
            if QXS[t] == "s":
                bundle("s", [i_act(R("QX", 2048 * h + k, 2048 * h + 2048, 16), R(Q, 128 * h, 128 * h + 128), F.Copy) for k in range(16)])
            else:
                bundle("v", [i_copy(R("QX", 2048 * h + k, 2048 * h + 2048, 16), R(Q, 128 * h, 128 * h + 128)) for k in range(16)])
        if t > 0:
            HUE[0] = 2
            for h in range(2):
                a, b = 128 * h, 128 * h + 128
                sact(R("N4V", a, b), R("VN", a, b), F.Copy, scale=4096.0)
                vcopy(R("V16", a, b), R("VN", a, b))
                dedupe("V16", lambda m: R("VU", m, m + 1), "EDV", "EQV", "ps7", 256, h, R("N4V", a, b), R("ps3", 256 + a, 256 + b))
            target(0, 16, "ps7", 256, "WCV", "TV1", "TV2", "TV3", lambda c0, c1: R("VU", c0, c1), "DWV", "VA")
        cb = lambda h: "ps%d" % (4 + h)

        def score(h, part):
            for w, (kc, g8) in enumerate((("KC1", "G8S"), ("KC2", "N8S"))):
                c = 128 * w
                pe([(R(cb(h), c, c + 128), R("ONES"), R(kc), True, False)] +
                   [(R(cb(h), c + k, c + 128, 16), part(k), R(g8), False, k == 15) for k in range(16)])
        for f in range(4):
            for h in range(2):
                HUE[0] = h
                lst = (IND("X", 4096, "DL", 128 * h, 128 * h + 128) if f == 0 else IND("X", 4096, "NL%s%d" % ("abc"[f - 1], h)))
                if f == 1:
                    d = IND("X", 4096, "DL", 128 * h, 128 * h + 128)
                    if SMODE[h] == "s":
                        sact(R("XG%d" % h), d, F.Copy)
                        for c in range(4):
                            bk = ("ps2", "ps6")[turn[0] % 2]
                            turn[0] += 1
                            mm = []
                            for kk in range(4):
                                reg = R(bk, 128 * kk, 128 * kk + 128)
                                mm += [(reg, R("I16"), R("XG%d" % h, 4 * c + kk, 2048, 16), True, False), (reg, R("NI"), R(Q, 128 * h, 128 * h + 128), False, True)]
                            pe(mm)
                            sact(R("AB%d" % h, 512 * c, 512 * c + 512), R(bk), F.Abs)
                        score(h, lambda k: R("AB%d" % h, 128 * k, 128 * k + 128))
                    else:
                        vtt(R("XG%d" % h), d, R("QX", 2048 * h, 2048 * h + 2048), A.subtract)
                        sact(R("AB%d" % h), R("XG%d" % h), F.Abs)
                        score(h, lambda k: R("AB%d" % h, k, 2048, 16))
                if f < 3:
                    ig = "IG%s%d" % ("ab"[f % 2], h)
                    nb = "ps%d" % h
                    for l0 in range(0, 128, CH):
                        l1 = l0 + CH
                        sact(R(ig, 16 * l0, 16 * l1), IND("M", 4096, "DL", 128 * h + l0, 128 * h + l1) if f == 0 else IND("M", 4096, "NL%s%d" % ("abc"[f - 1], h), l0, l1), F.Copy)
                        pe([(R(nb, 320 + l0, 320 + l1), R("LK", 128 * k, 128 * k + 128), R(ig, 16 * l0 + k, 16 * l1, 16), k == 0, k == 15) for k in range(16)])
                        vcopy(R("NL%s%d" % ("abc"[f], h), l0, l1), R(nb, 320 + l0, 320 + l1))
                if f > 0:
                    lw = "LW%s%d" % ("aba"[f - 1], h)
                    for l0 in range(0, 128, CH):
                        l1 = l0 + CH
                        vtt(R(lw, 16 * l0, 16 * l1), IND("X", 4096, "NL%s%d" % ("abc"[f - 1], h), l0, l1), R("QX", 2048 * h + 16 * l0, 2048 * h + 16 * l1), A.is_lt)
                    pe([(R(cb(h), 384 + k, 512, 16), R(lw, k, 2048, 16), R("G8"), True, True) for k in range(16)])
                    if f == 1:
                        sact(R("M1%d" % h), R(cb(h), 384, 512), F.Copy)
                    if f == 2:
                        vtt(R("M2%d" % h), R(cb(h), 384, 512), R("M1%d" % h), A.max)
        for h in range(2):
            a, b = 128 * h, 128 * h + 128
            H = str(h)
            HUE[0] = h
            s1, at, mb = R(cb(h), 0, 128), R(cb(h), 128, 256), "ps%d" % h
            vtt(R("M3" + H), R(cb(h), 384, 512), R("M2" + H), A.max)
            vts(R("CL" + H), R("M3" + H), 8.5, None, A.is_ge)
            vtt(R("UU" + H), R("CL" + H), at, A.mult)
            vtt(R("KEY" + H), R("UU" + H), s1, A.max)
            vscan(R("SCN" + H), R("DMIN"), R("KEY" + H), A.max, A.min)
            bundle("v", [i_ts(R("OHT" + H, k, k + 16), R("KEY" + H, k, k + 16), R("SCN" + H, k + 15, k + 16), None, A.is_equal) for k in range(0, 128, 16)])
            pe([(R(mb, 0, 128), R("OHT" + H), R("I16"), True, True)])
            vtt(R("UD" + H), R("DF", a, b), R(mb, 0, 128), A.mult)
            pe([(R(mb, 320, 448), R("BOF"), R("UD" + H), True, True)], 4)
            own(R("WS0" + H), R(mb, 320, 448))
            vts(R("AL0" + H), R("WS0" + H, 15, 128, 16), R("SC1"), -1.0, A.mult, A.add)
            vcopy(R("HD" + H, 3, 32, 4), R("WS0" + H, 15, 128, 16))
            vts(R("NB", 8 * h, 8 * h + 8), R("SCN" + H, 15, 128, 16), BIG, None, A.is_ge)
            sact(R(mb, 128, 256), R(mb, 0, 128), F.Identity, bias=1.0, scale=-1.0)
            vtt(R("ND", a, b), R("DF", a, b), R(mb, 128, 256), A.mult)
            if h == 1:
                pe([(R(mb, 304, 320), R("ONES"), R("NB"), True, True)])
                node("v", [lambda: V.tensor_reduce(ap(R("NR")), ap(R("ps1", 304, 320)), X, A.add)], [R("ps1", 304, 320)], [R("NR")], 64 * CY)
                vcopy(R("NRi"), R("NR"))
                vts(R("NA"), R("NRi"), 255, None, A.bitwise_and)
                vts(R("AH"), R("NA"), 0.5, -0.25, A.mult, A.add)
                sact(R("ZI"), R(Q), F.Identity, bias=R("AH"), scale=0.5)
                sact(R("ZI"), R("ZI"), F.Identity, bias=MAGIC)
                sact(R("ZB", 256 * t, 256 * t + 256), R("ZI"), F.Identity, bias=-MAGIC)
                send("z", "ZB", 256 * t, 256 * t + 256, "RZ", t)
            for s in range(1, 4):
                prev = "AL%d%s" % (s - 1, H)
                sact(R("WM%d" % s + H), IND("PV1", 4096, prev), F.Copy)
                own(R("WS%d" % s + H), R("WM%d" % s + H))
                vts(R("AL%d" % s + H), R("WS%d" % s + H, 15, 128, 16), R("SC1"), -1.0, A.mult, A.add)
                vtt(R("LQ" + H, 128 * s - 128, 128 * s), IND("X", 4096, "AL%d" % s + H), R(Q, a, b), A.is_lt)
            vtt(R("HD" + H, 2, 32, 4), R("WS1" + H, 15, 128, 16), R("HD" + H, 3, 32, 4), A.subtract)
            vtt(R("HD" + H, 1, 32, 4), R("WS2" + H, 15, 128, 16), R("WS1" + H, 15, 128, 16), A.subtract)
            vtt(R("HD" + H, 0, 32, 4), R("WS3" + H, 15, 128, 16), R("WS2" + H, 15, 128, 16), A.subtract)
            pe([(R(mb, 272, 296), R("LB", 128 * k, 128 * k + 128), R("LQ" + H, k, 384, 16), k == 0, k == 15) for k in range(16)])
            bundle("v", [i_ts(R("HG" + H, 4 - s, 32, 4), R(mb, 264 + 8 * s, 272 + 8 * s), 8.5, None, A.is_lt) for s in range(1, 4)])
            vscan(R("HS" + H), R("HG" + H), R("HD" + H), A.mult, A.add)
            vts(R("AL", 8 * h, 8 * h + 8), R("HS" + H, 3, 32, 4), R("SC1"), -1.0, A.mult, A.add)
            vts(R("HU", 8 * h, 8 * h + 8), R("HS" + H, 3, 32, 4), R("SC1"), None, A.mult)
            al = (8 * h, 8 * h + 8)
            sact(R("WB", 256 * t + a, 256 * t + b), IND("RC1", 4096, "AL", *al), F.Copy)
            send("ab"[h], "WB", 256 * t + a, 256 * t + b, "RV", t)
            sact(R("NAT", a, b), IND("IO1", 4096, "AL", *al), F.Copy)
            vcopy(R("A16", a, b), R("NAT", a, b))
            sact(R("N4A", a, b), R("NAT", a, b), F.Copy, scale=4096.0)
            own(R("ps3", a, b), R("NAT", a, b))
            vtt(R("UT", a, b), R("NAT", a, b), R(mb, 0, 128), A.mult)
            vtt(R("XS", a, b), IND("X", 4096, "AL", *al), R(Q, a, b), A.add)
            sact(R("XS", a, b), R("XS", a, b), F.Identity, bias=0.25, scale=0.5)
            sact(R("XS", a, b), R("XS", a, b), F.Identity, bias=MAGIC)
            sact(R("XS", a, b), R("XS", a, b), F.Identity, bias=-MAGIC)
            if t < RO - 1:
                sact(R("NP", a, b), IND("M", 4096, "AL", *al), F.Copy)
                pe([(R("ps%d" % h, 448, 456), R("LK", 128 * k, 128 * k + 128), R("NP", a + k, b, 16), k == 0, k == 15) for k in range(16)])
                vcopy(R("NLA", *al), R("ps%d" % h, 448, 456))
                sact(R("NNP", a, b), IND("M", 4096, "NLA", *al), F.Copy)
            dedupe("A16", lambda m: R("HU", m, m + 1), "EDA" + H, "EQA" + H, "ps7", 0, h, R("N4A", a, b), R("ps3", a, b))
        target(0, 16, "ps7", 0, "WCA", "TA1", "TA2", "TA3", lambda c0, c1: R("HU", c0, c1), "DWA", "ADR")
        HUE[0] = 2
        if t < RO - 1:
            vcopy(IND("M", 4352, "ADR"), R("NNP"))
        vcopy(IND("X", 4352, "ADR"), R("XS"))
        vtt(IND("U", 1280, VA), R("ND"), R("UT"), A.add)
    dma("y", [(lambda: T.yx[:, :], lambda: ap(R("X", 0, 4096)))], [R("X", 0, 4096)], [], 1048576)
    vts(R("U", 0, 512), R("U", 0, 512), -1.0, None, A.add)
    sact(R("U", 512, 1024), R("U", 512, 1024), F.Identity, bias=-1.0)
    dma("y", [(lambda: T.yu[:, :], lambda: ap(R("U", 0, 1024)))], [R("U", 0, 1024)], [], 524288)
    o = 256 * (RO - 1)
    bundle("v", [i_ts(R("YV", 0, 256, 2), R("WB", o, o + 256, 2), -1.0, None, A.add), i_ts(R("YV", 1, 256, 2), R("RV", o + 1, o + 256, 2), -1.0, None, A.add)])
    Q = "Q%d" % (RO % 2)
    bundle("v", [i_copy(R(Q, 0, 256, 2), R("ZB", o, o + 256, 2)), i_copy(R(Q, 1, 256, 2), R("RZ", o + 1, o + 256, 2))])
    py, oy = POOL["YV"]
    dma("y", [(lambda: T.yv[:, :], lambda: T[py][0:128:16, oy:oy + 256])], [R("YV")], [], 8192)
    dma("y", [(lambda: T.yq[:, :], lambda: ap(R(Q)))], [R(Q)], [], 65536)

    emit(g, T, nodes)


def schedule(nodes, hint):
    N = len(nodes)
    succ = [[] for _ in nodes]
    for i, n in enumerate(nodes):
        for j in n["need"] | n["order"]:
            succ[j].append(i)
    prio = [0.0] * N
    for i in range(N - 1, -1, -1):
        n = nodes[i]
        prio[i] = n["cost"] + n["lat"] + HOP + max([prio[k] for k in succ[i]] + [0.0])
    prio = [p + hint.get(n["lab"][1], 0.0) + hint.get(n["lab"], 0.0) for p, n in zip(prio, nodes)]
    left = [len(n["need"] | n["order"]) for n in nodes]
    ready = [0.0] * N
    avail = {}
    free = {}
    for i, n in enumerate(nodes):
        if not left[i]:
            avail.setdefault(n["q"], []).append(i)
    order = []
    while len(order) < N:
        best = None
        for q, L in avail.items():
            if not L:
                continue
            f = 0.0 if q == "net" else free.get(q, 0.0)
            s = max(f, min(ready[i] for i in L))
            c = max((i for i in L if ready[i] <= s), key=lambda i: prio[i])
            if best is None or s < best[0]:
                best = (s, q, c)
        s, q, c = best
        avail[q].remove(c)
        n = nodes[c]
        free[q] = s + n["cost"]
        e = s + n["cost"] + n["lat"]
        order.append(c)
        for k in succ[c]:
            left[k] -= 1
            ready[k] = max(ready[k], e + (HOP if c in nodes[k]["need"] else 0.0))
            if not left[k]:
                avail.setdefault(nodes[k]["q"], []).append(k)
    return order, max(free.values())


def emit(g, T, nodes):
    order, _ = schedule(nodes, HINT)
    eng = {"v": g.vector, "s": g.scalar, "t": g.tensor, "g": g, "y": g.sync}
    count, known, after, tok = {}, {q: {} for q in eng}, {}, {}
    sent = 0

    def wait(q, k, v):
        eng[q].wait_ge(T.sem[k], v)
        known[q][k] = v
    for i in order:
        n = nodes[i]
        q = n["q"]
        if q == "net":
            tok[i] = (n["rsem"], n["tot"])
            after[i] = {n["rsem"]: n["tot"]}
            continue
        K = known[q]
        ds = [d for d in n["need"] if "remote" not in nodes[d]]
        todo = {}
        for d in ds:
            k, v = tok[d]
            if K.get(k, 0) < v and todo.get(k, (0, 0))[0] < v:
                todo[k] = (v, d)
        for k in list(todo):
            v, d = todo[k]
            if any(k2 != k and after[d2].get(k, 0) >= v for k2, (v2, d2) in todo.items()):
                del todo[k]
        for k, (v, d) in sorted(todo.items()):
            wait(q, k, v)
        for k, (v, d) in todo.items():
            for k2, v2 in after[d].items():
                K[k2] = max(K.get(k2, 0), v2)
        if "remote" in n:
            n["calls"][0]()
            sent += n["remote"]
        elif "dsem" in n:
            for c in n["calls"]:
                c().then_inc(T.sem[n["dsem"]], 16)
            tok[i] = (n["dsem"], n["tot"])
            after[i] = dict(K)
            after[i][n["dsem"]] = n["tot"]
        else:
            for c in n["calls"]:
                c().then_inc(T.sem["q" + q], 1)
            count[q] = count.get(q, 0) + len(n["calls"])
            tok[i] = ("q" + q, count[q])
            after[i] = dict(K)
            after[i]["q" + q] = count[q]
    for q in "vstg":
        if known["y"].get("q" + q, 0) < count.get(q, 0):
            wait("y", "q" + q, count[q])
    for n in nodes:
        if "dsem" in n and known["y"].get(n["dsem"], 0) < n["tot"]:
            wait("y", n["dsem"], n["tot"])
        if "rsem" in n and known["y"].get(n["rsem"], 0) < n["tot"]:
            wait("y", n["rsem"], n["tot"])
    g.wait_ge(T.sem.ls, sent)
